import numpy as np, ml_dtypes
CORES = [2,6,10,14,18,22,26,30]
N = 8
BF = ml_dtypes.bfloat16
W, C, TS, S = 4096, 128, 5, 3
B = W // C
SHAPES = np.array([[0, 15, 1, 2, 3, 4, 5, 6, 7, 8, 9, 10, 11, 12, 13, 14], [0, 1, 2, 15, 3, 14, 4, 13, 5, 12, 6, 11, 7, 10, 8, 9], [14, 15, 0, 13, 1, 12, 2, 11, 3, 10, 4, 9, 5, 8, 6, 7],
                   [1, 14, 0, 15, 2, 3, 4, 5, 6, 7, 8, 9, 10, 11, 12, 13], [7, 8, 0, 15, 1, 14, 2, 13, 3, 12, 4, 11, 5, 10, 6, 9], [3, 11, 0, 8, 1, 9, 2, 10, 4, 12, 5, 13, 6, 14, 7, 15],
                   [0, 2, 1, 3, 4, 15, 5, 14, 6, 13, 7, 12, 8, 11, 9, 10]])
def place(a, b, n):
    return ((a * b >> 5) + 37 * a + 11 * b + (n & 63)) & (W - 1)
def mate(o):
    p = np.zeros_like(o); np.put_along_axis(p, o, o[..., np.array([0, 1, 3, 2, 5, 4, 7, 6, 9, 8, 11, 10, 13, 12, 15, 14])], -1)
    return np.ascontiguousarray(np.moveaxis(p, -1, -2))
def loose(p):
    m = p == np.arange(16).reshape(1, 1, 16, 1)
    return np.argmax(m, axis=2), 15 - np.argmax(m[:, :, ::-1], axis=2)
def look(x, l, p, fr, z, a):
    lf = np.take_along_axis(l, fr[:, :, None, :], 2); lp = np.take_along_axis(l, p, 2); n = a[:, :, None, None]
    xk = np.take_along_axis(x, place(l, lp, n).reshape(N, 8, 1, 16 * C), 3).reshape(N, 8, 16, 16, C)
    yk = np.take_along_axis(x, place(lf, l, n).reshape(N, 8, 1, 16 * C), 3).reshape(N, 8, 16, 16, C)
    dx = np.sum(np.abs(xk - z[:, :, :, None, :]), axis=2); dy = np.sum(np.abs(yk - z[:, :, :, None, :]), axis=2)
    return xk, yk, dx, dx - dy
def parts(rng):
    x = rng.integers(0, 64, (N, 8, 16, W)); l = rng.integers(0, 4096, (N, 8, 16, C)); z = rng.integers(0, 64, (N, 8, 16, C))
    p = mate(np.argsort(rng.random((N, 8, C, 16)), axis=-1)); t = rng.integers(60, 241, (N, 8, TS))
    return x, l, p, z, t
def pack(x, l, p, z, t):
    return {"xt": np.ascontiguousarray(x.reshape(N, 128, W)).astype(np.float32).astype(BF), "nm": np.ascontiguousarray(l.reshape(N, 128, C)).astype(np.int32),
            "pr": np.ascontiguousarray(p.reshape(N, 128, C)).astype(np.int32), "z0": np.ascontiguousarray(z.reshape(N, 128, C)).astype(np.float32).astype(BF),
            "th": np.ascontiguousarray(np.repeat(t, 16, axis=1)).astype(np.int32)}
def plant(rng, x, l, p, z, used, q, g, i, zz, v, w, odd, last):
    c = rng.integers(0, 4096, (512, 16)); pp = p[q, g, :, i]; bd = np.flatnonzero(pp != np.arange(16)); fr = int(np.flatnonzero(pp == np.arange(16))[0])
    hx = place(c[:, bd], c[:, pp[bd]], 0); hy = place(c[:, fr:fr + 1], c[:, bd], 0); h = np.concatenate([hx, hy], axis=1); k = np.sort(h, axis=1)
    fit = np.all(k[:, 1:] != k[:, :-1], axis=1) & ~np.any(used[h], axis=1); j = int(np.argmax(fit))
    assert fit[j], "no fitting names"
    ax = np.zeros((16, len(bd)), np.int64) + np.reshape(v, (-1, 1)); ax[15, :-1] = odd; ax[15, -1] = last
    xx = x[q, g]; xx[:, hx[j]] = ax; xx[:, hy[j]] = w
    l[q, g, :, i] = c[j]; z[q, g, :, i] = zz; used[h[j]] = True
def setup_inputs(rng):
    return pack(*parts(rng))
def setup_inputs_spread(rng):
    x, l, p, z, t = parts(rng)
    x = (rng.random((N, 8, 16, W)) * np.exp2(rng.integers(0, 7, (N, 8, 1, W)))).astype(np.int64); x = np.where(rng.random((N, 8, 1, W)) < 0.5, 63 - x, x)
    l = np.where(rng.random((N, 8, 1, C)) < 0.5, np.exp2(12 * rng.random((N, 8, 16, C))).astype(np.int64) - 1, l); l = np.minimum(l, 4095)
    z = np.where(rng.random((N, 8, 1, C)) < 0.7, np.minimum(np.exp2(6 * rng.random((N, 8, 16, C))).astype(np.int64) - 1, 63), z)
    t = np.where(rng.random((N, 8, TS)) < 0.4, rng.integers(-1008, 1009, (N, 8, TS)), rng.integers(0, 300, (N, 8, TS)))
    return pack(x, l, p, z, t)
def setup_inputs_ends(rng):
    x, l, p, z, t = parts(rng)
    x = 63 * np.where(rng.random((N, 8, 1, W)) < 0.75, rng.integers(0, 2, (N, 8, 1, W)), rng.integers(0, 2, (N, 8, 16, W)))
    l = np.where(rng.random((N, 8, 16, C)) < 0.75, 4095 * rng.integers(0, 2, (N, 8, 16, C)), l)
    z = 63 * np.where(rng.random((N, 8, 1, C)) < 0.6, rng.integers(0, 2, (N, 8, 1, C)), rng.integers(0, 2, (N, 8, 16, C)))
    sh = rng.integers(0, 6, (N, 8, C)); sh[:, :, np.array([0, C // 2, C - 1])] = 1
    sh[:, :, np.array([1, 2, C - 3])] = 6; sh[1::2, :, C // 2] = 6; p = mate(SHAPES[sh])
    t = 2016 * rng.integers(0, 2, (N, 8, TS)) - 1008; t[:, 0] = 1008; t[:, 1] = -1008
    t[:, 2] = rng.choice(np.array([1007, 0, -1007, 500]), (N, TS)); t[:, 5] = rng.choice(np.array([1007, 0, -1007, 500]), (N, TS))
    t[:, 2, 0] = 1007; t[:, 5, 0] = 1007; t[:, 7, 0] = 1007
    for q in range(N):
        for g in range(8):
            used = np.zeros(W, bool); m = int(rng.integers(9, 16))
            plant(rng, x, l, p, z, used, q, g, C - 1, 63, 0, 63, 1, 0)
            plant(rng, x, l, p, z, used, q, g, C - 2, 0, 0, 63, 0, 0)
            plant(rng, x, l, p, z, used, q, g, 0, 63, 63, 0, 62, 63)
            plant(rng, x, l, p, z, used, q, g, C // 2, 63, 0, 63, 0, 0)
            plant(rng, x, l, p, z, used, q, g, 1, 63, 0, 0, 0, 1)
            plant(rng, x, l, p, z, used, q, g, C - 3, 63, 63, 0, 63, 62)
            plant(rng, x, l, p, z, used, q, g, 2, 63, np.where(np.arange(16) < m, 0, 63), 0, 62, 63)
    return pack(x, l, p, z, t)
def setup_inputs_corners(rng):
    x, l, p, z, t = parts(rng); p = mate(SHAPES[rng.integers(0, 6, (N, 8, C))])
    l[:, 0] = rng.integers(0, 4096, (N, 1, C)); t[:, 0] = rng.integers(-1, 1, (N, TS))
    for q in range(N): l[q, 1] = (0, 4095, 1, 2048, 4094, 77, 1023, 64)[(q + int(rng.integers(0, 8))) % 8]
    l[:, 2] = 4095 * rng.integers(0, 2, (N, 16, C))
    x[:, 3] = rng.integers(0, 64, (N, 16, 1)); t[:, 3] = rng.integers(-1, 1, (N, TS))
    z[:, 4] = 63 * rng.integers(0, 2, (N, 1, C))
    t[:, 7] = 2016 * rng.integers(0, 2, (N, TS)) - 1008
    fr, e = loose(p); s = look(x, l, p, fr, z, np.zeros((N, 8), np.int64))[3]
    best = np.max(np.where(p != np.arange(16).reshape(1, 1, 16, 1), s, -1008), axis=2)
    t[:, 5, 0] = best[:, 5, 0]; t[:, 6, 0] = np.maximum(best[:, 6, C - 1] - 1, -1008)
    return pack(x, l, p, z, t)
def setup_inputs_crowd(rng):
    x, l, p, z, t = parts(rng); x = rng.integers(1, 63, (N, 8, 16, W)); z = rng.integers(1, 63, (N, 8, 16, C))
    l[:, 4] = rng.integers(0, 4096, (N, 1, 1)); l[:, 6] = rng.integers(0, 4096, (N, 1, 1))
    t[:] = 1008; t[:, 1, 0] = 1007; t[:, 5, 0] = 1007
    for g in (2, 3, 6, 7): t[:, g] = -1008
    for q in range(N):
        for g, i in ((1, C - 1), (5, 0)): plant(rng, x, l, p, z, np.zeros(W, bool), q, g, i, 63, 0, 63, 0, 0)
        for g, i in ((3, 0), (7, C - 1)): plant(rng, x, l, p, z, np.zeros(W, bool), q, g, i, 0, 0, 63, 0, 0)
    return pack(x, l, p, z, t)
def check_inputs(d):
    bad = []
    for k, lo, hi in (("xt", 0, 63), ("nm", 0, 4095), ("pr", 0, 15), ("z0", 0, 63), ("th", -1008, 1008)):
        v = np.asarray(d[k]).astype(np.float64)
        if not (np.min(v) >= lo and np.max(v) <= hi): bad.append("range of " + k)
        elif np.any(v != np.floor(v)): bad.append("whole numbers in " + k)
    p = np.clip(np.asarray(d["pr"]).astype(np.int64), 0, 15).reshape(N, 8, 16, C); row = np.arange(16).reshape(1, 1, 16, 1)
    if np.any(np.take_along_axis(p, p, 2) != row): bad.append("pairs in pr")
    if np.any(np.sum(p == row, axis=2) != 2): bad.append("two free rows in pr")
    t = np.asarray(d["th"]).reshape(N, 8, 16, TS)
    if np.any(t != t[:, :, :1]): bad.append("rows of a group alike in th")
    return bad
def reference(xt, nm, pr, z0, th):
    x = xt.astype(np.float32).astype(np.int64).reshape(N, 8, 16, W); l = nm.astype(np.int64).reshape(N, 8, 16, C); p = pr.astype(np.int64).reshape(N, 8, 16, C)
    z = z0.astype(np.float32).astype(np.int64).reshape(N, 8, 16, C); tt = th.astype(np.int64).reshape(N, 8, 16, TS)[:, :, 0]
    row = np.arange(16).reshape(1, 1, 16, 1); fr, e = loose(p); a = np.zeros((N, 8), np.int64); ct = np.zeros((TS, N, 8), np.int64)
    for t in range(TS):
        at = (np.arange(N) + S * t) % N; xa = x[at]
        xk, yk, dx, s = look(xa, l, p, fr, z, a[at]); bonded = p != row
        top = np.where(bonded, s, -9999); k1 = np.argmax(top, axis=2); k2 = np.argmin(np.where(bonded, dx, 9999), axis=2)
        esc = np.max(top, axis=2) <= tt[at][:, :, t:t + 1]
        k = np.where(esc, k2, k1); kk = k[:, :, None, :]; q = np.take_along_axis(p, kk, 2); es = esc[:, :, None, :]
        px = np.take_along_axis(xk, k[:, :, None, None, :], 3)[:, :, :, 0]; py = np.take_along_axis(yk, k[:, :, None, None, :], 3)[:, :, :, 0]
        z = np.where(es, np.abs(z - px), (z + py) >> 1)
        ff = fr[:, :, None, :]; m = np.where(es, e[:, :, None, :], kk)
        p = np.where(row == ff, m, np.where(row == m, ff, p)); p = np.where(row == q, q, p); p = np.where(es & (row == kk), kk, p)
        q = q[:, :, 0]; fr = np.where(esc, k, q); e = np.where(esc, q, e)
        col = (B * np.arange(C) + (np.sum(z, axis=2) & (B - 1)))[:, :, None, :]
        new = (np.take_along_axis(xa, col, 3) + z) >> 1
        np.put_along_axis(xa, np.ascontiguousarray(np.broadcast_to(col, (N, 8, 16, C))), new, 3); x[at] = xa
        ct[t, at] = np.sum(esc, axis=2); a = a + ct[t]
    return {"yx": x.reshape(N, 128, W).astype(np.float32).astype(BF), "ye": np.ascontiguousarray(np.repeat(np.moveaxis(ct, 0, -1), 16, axis=1)).astype(np.float32),
            "yp": p.reshape(N, 128, C).astype(np.float32), "yf": fr.astype(np.float32), "yz": z.reshape(N, 128, C).astype(np.float32).astype(BF)}

@@ -1,0 +1,451 @@
+from concourse.bass import DstId, RemoteDMATransfer
+from concourse.mybir import dt, AluOpType, AxisListType, ActivationFunctionType
+
+TS, N, HOP = 5, 8, 3
+F32, BF, I32, U16 = "float32", "bfloat16", "int32", "uint16"
+
+
+def _sb(n, d):
+    return ("sbuf", [128, n], d)
+
+
+SCRATCH = {
+    "X": _sb(4096, BF), "W2": _sb(3840, BF), "DX": _sb(1792, BF), "AY": _sb(1792, BF),
+    "NMI": _sb(128, I32), "PRI": _sb(128, I32), "Z0": _sb(128, BF), "THI": _sb(8, I32), "TH": _sb(8, F32),
+    "PI": _sb(8, I32), "PJ": _sb(8, I32), "COL": _sb(16, F32), "J": _sb(144, F32), "GI": _sb(128, F32),
+    "Q": _sb(144, BF), "Q2": _sb(144, BF), "ID": _sb(128, BF), "IA": _sb(128, BF), "IB": _sb(128, BF), "IF": _sb(128, F32),
+    "BO": _sb(128, BF), "LT1": _sb(128, BF), "LT2": _sb(128, BF), "LTF": _sb(128, F32),
+    "HI": _sb(128, I32), "LO": _sb(128, I32), "HIB": _sb(128, BF), "LOB": _sb(128, BF), "NZ": _sb(2048, BF), "CL": _sb(2048, BF),
+    "LF": _sb(256, BF), "MM": _sb(256, BF), "W16": _sb(128, BF), "WK": _sb(128, BF), "WP": _sb(128, BF), "PB": _sb(128, BF),
+    "PN1": _sb(128, F32), "PN2": _sb(128, F32), "RN": _sb(128, F32), "ON": _sb(128, U16),
+    "PTX": _sb(112, BF), "PTY": _sb(112, BF), "PAT": _sb(224, F32), "RST": _sb(224, F32), "CB": _sb(8, F32),
+    "JJ": _sb(16, F32), "QI": _sb(16, I32), "QW": _sb(16, I32), "QF": _sb(16, F32), "QG": _sb(16, F32), "C2": _sb(8, F32), "C512": _sb(8, F32),
+    "LFE": _sb(16, U16), "LC": _sb(16, U16), "LTP": _sb(16, U16), "L12": _sb(16, U16),
+    "RP": _sb(128, BF), "WA": _sb(128, F32), "BL": _sb(112, F32), "HP": _sb(224, I32), "OFF": _sb(224, U16),
+    "K2": _sb(112, F32), "K1": _sb(120, F32), "MI": _sb(8, I32), "M2": _sb(8, I32), "C": _sb(16, I32), "OZ": _sb(8, U16),
+    "TT": _sb(224, F32), "MK": _sb(224, F32), "DW": _sb(448, F32), "TZ": _sb(128, F32),
+    "UI": _sb(8, I32), "CU": _sb(8, U16), "TA": _sb(128, BF), "M129": _sb(128, BF), "EB": _sb(8, BF), "EJ": _sb(8, F32),
+    "YE": _sb(8, F32), "AI": _sb(4, I32), "A63": _sb(4, F32),
+    "IH": _sb(256, BF), "IL": _sb(256, BF), "ID2": _sb(272, BF), "R16": _sb(128, F32), "R1": _sb(128, F32), "CC": _sb(128, F32),
+    "OP": _sb(136, U16), "YP": _sb(128, F32), "YF": _sb(128, F32), "YZ": _sb(128, BF), "ZF": _sb(128, BF),
+    "IF2": _sb(128, F32), "PN3": _sb(128, F32), "DG": _sb(128, BF), "R16S": _sb(128, F32), "US": _sb(128, F32), "G2": _sb(896, BF),
+    "SL": _sb(128 * (TS + 1), F32), "PL": _sb(128 * (TS + 1), F32), "CI": _sb(16 * (TS + 1), I32), "CO": _sb(16 * TS, I32),
+}
+for _t in range(TS):
+    SCRATCH["W1_%d" % _t] = _sb(3840, BF)
+    SCRATCH["ZN_%d" % _t] = _sb(128, BF)
+for _t in range(8):
+    SCRATCH["B%d" % _t] = ("psum", [128, 512], F32)
+
+SEMAPHORES = (["cV", "cS", "cP", "cG", "left"] + ["d%d" % i for i in range(24)]
+              + ["a%s%d" % (k, i) for k in "zsc" for i in range(TS)])
+
+A = AluOpType
+AF = ActivationFunctionType
+MAGIC = float(3 * 2 ** 35)
+
+
+def rank_program(g, core, T, topo):
+    rank = T.rank_of(core)
+    if rank is None:
+        return
+    Q = {"V": g.vector, "S": g.scalar, "P": g.tensor, "G": g, "Y": g.sync}
+    ops = []
+
+    def op(q, fn, r=(), w=(), dma=None):
+        ops.append({"q": q, "fn": fn, "r": list(r), "w": list(w), "dma": dma, "kind": "op"})
+
+    def arrive(sem, n, w):
+        ops.append({"q": None, "r": [], "w": list(w), "kind": "ext", "sem": sem, "n": n, "dma": None})
+
+    def ts(out, in0, s1, s2, o0, o1, r, w):
+        if o1 is None:
+            op("V", lambda: g.vector.tensor_scalar(out, in0, s1, None, o0), r, w)
+        else:
+            op("V", lambda: g.vector.tensor_scalar(out, in0, s1, s2, o0, o1), r, w)
+
+    def tt(out, in0, in1, o, r, w):
+        op("V", lambda: g.vector.tensor_tensor(out, in0, in1, o), r, w)
+
+    def cp(out, in_, r, w):
+        op("V", lambda: g.vector.tensor_copy(out, in_), r, w)
+
+    def ms(out, c, w):
+        op("V", lambda: g.vector.memset(out, c), [], w)
+
+    def act(out, in_, f, r, w, bias=0.0, scale=1.0, acc=None):
+        if acc is None:
+            op("S", lambda: g.scalar.activation(out, in_, f, bias=bias, scale=scale), r, w)
+        else:
+            op("S", lambda: g.scalar.activation(out, in_, f, bias=bias, scale=scale, accum_out=acc), r, w)
+
+    def mm(out, l, rh, st, sp, r, w):
+        op("P", lambda: g.tensor.matmul(out, l, rh, st, sp), r, w)
+
+    def iota(out, pat, base, cm, w, isint=False):
+        if isint:
+            op("G", lambda: g.iota(out, pat, base, cm), [], w)
+        else:
+            op("G", lambda: g.iota(out, pat, base, cm, allow_small_or_imprecise_dtypes=True), [], w)
+
+    def dma(q, out, in_, r, w, grp):
+        op(q, lambda: Q[q].dma_start(out, in_), r, w, dma=grp)
+
+    def fold(bank, n, sel, data, c0, r, first):
+        for b in range(16):
+            mm(T[bank][:, 0:n], sel[:, 15 - b:143 - b], data[:, c0 + b:c0 + 16 * n:16], first and b == 0, b == 15, r, [bank])
+
+    W1 = [T["W1_%d" % t] for t in range(TS)]
+    left = [0]
+
+    def send(t, kind, dst, src, r):
+        to = T.cores[(rank + (HOP if t < TS - 1 else -HOP * (TS - 1))) % N]
+        rid, pid, _ = topo.addr(to)
+        mask = topo.mask(core, to)
+        left[0] += len(topo.engines(core, to))
+        op("G", lambda: g.remote_dma(dst, src, T.sem["a%s%d" % (kind, t)], T.sem.left, pid, rid, mask), r, [], dma="remote")
+
+    def landed(t, kind, key):
+        frm = T.cores[(rank - (HOP if t < TS - 1 else -HOP * (TS - 1))) % N]
+        arrive("a%s%d" % (kind, t), len(topo.engines(frm, core)), [key])
+
+    col = lambda j: T.COL[:, j:j + 1]
+
+    dma("Y", T.PRI[:], T.pr[:], [], ["PRI"], "pr")
+    dma("S", T.NMI[:], T.nm[:], [], ["NMI"], "nm")
+    dma("S", T.Z0[:], T.z0[:], [], ["Z0"], "z0")
+    dma("S", T.THI[:, 0:TS], T.th[:], [], ["THI"], "th")
+    dma("Y", T.X[:, 0:2048], T.xt[:, 0:2048], [], ["X"], "x")
+    dma("Y", T.X[:, 2048:4096], T.xt[:, 2048:4096], [], ["X"], "x")
+
+    iota(T.PI[:, 0:1], [[0, 1]], 0, 1, ["PI"], True)
+    iota(T.J[:], [[1, 144]], 0, -1, ["J"])
+    iota(T.GI[:], [[1, 8], [0, 16]], 0, 0, ["GI"])
+    iota(T.PN1[:, 0:112], [[0, 2], [1920, 7], [-1, 8]], 3072, 0, ["PN1"])
+    iota(T.PN1[:, 112:128], [[1920, 2], [-1, 8]], 1920 * 8 + 1152, 0, ["PN1"])
+    iota(T.PN2[:, 0:64], [[0, 64]], -2, 0, ["PN2"])
+    iota(T.PN3[:], [[0, 16], [1024, 8]], 0, 0, ["PN3"])
+    iota(T.JJ[:], [[16, 16]], 0, 0, ["JJ"])
+    iota(T.C2[:], [[2, 8]], 0, 0, ["C2"])
+    iota(T.C512[:], [[512, 8]], 0, 0, ["C512"])
+    iota(T.PTX[:], [[8, 14], [1, 8]], 128, 0, ["PTX"])
+    iota(T.PTY[:], [[0, 2], [16, 7], [2, 8]], 184, 0, ["PTY"])
+    iota(T.PAT[:, 0:112], [[1, 8], [8, 14]], 0, 0, ["PAT"])
+    iota(T.PAT[:, 112:224], [[1, 8], [-56, 2], [8, 7]], 184, 0, ["PAT"])
+    iota(T.RST[:], [[0, 16], [1, 14]], 0, 0, ["RST0"])
+    iota(T.IH[:], [[1, 16], [0, 16]], 0, 0, ["IH"])
+    iota(T.IL[:], [[0, 16], [1, 16]], 0, 0, ["IL"])
+    iota(T.ID2[:, 256:272], [[1, 16]], 0, 0, ["ID2b"])
+    iota(T.R16S[:], [[0, 8], [1, 16]], 0, 0, ["R16S0"])
+    iota(T.M129[:], [[0, 128]], -129, 0, ["M129"])
+    iota(T.W2[:, 1792:3840], [[0, 2048]], 129, 0, ["W2c"])
+
+    ms(T.NZ[:], 0.0, ["NZ"])
+    ts(T.PJ[:, 0:1], T.PI[:, 0:1], 15, None, A.bitwise_and, None, ["PI"], ["PJ0"])
+    ts(T.PJ[:, 1:2], T.PI[:, 0:1], 4, None, A.arith_shift_right, None, ["PI"], ["PJ1"])
+    ts(T.PJ[:, 2:3], T.PI[:, 0:1], 7, None, A.bitwise_and, None, ["PI"], ["PJ2"])
+    ts(T.PJ[:, 3:4], T.PI[:, 0:1], 3, 1, A.arith_shift_right, A.bitwise_and, ["PI"], ["PJ3"])
+    cp(T.COL[:, 0:4], T.PJ[:, 0:4], ["PJ0", "PJ1", "PJ2", "PJ3"], ["c0"])
+    ts(T.LTF[:], T.J[:, 0:128], 0.0, 16.0, A.is_ge, A.mult, ["J"], ["LTF"])
+    ts(T.ID[:], T.J[:, 0:128], 0.0, None, A.is_equal, None, ["J"], ["ID"])
+    ts(T.BO[:], T.GI[:], col(1), None, A.is_equal, None, ["GI", "c0"], ["BO"])
+    ts(T.IF[:], T.J[:, 0:128], 0.0, 112.0, A.is_equal, A.mult, ["J"], ["IF"])
+    ts(col(4), col(0), -1.0, 15.0, A.mult, A.add, ["c0"], ["c4"])
+    tt(T.LT1[:], T.LTF[:], T.BO[:], A.mult, ["LTF", "BO"], ["LT1"])
+    ts(T.IF2[:], T.J[:, 0:128], 0.0, 1024.0, A.is_equal, A.mult, ["J"], ["IF2"])
+    tt(T.LT2[:], T.LT1[:], T.IF[:], A.add, ["LT1", "IF"], ["LT2"])
+
+    ts(T.LF[:, 0:128], T.PRI[:], col(0), None, A.is_gt, None, ["PRI", "c0"], ["LFa"])
+    ts(T.LF[:, 128:256], T.PRI[:], col(0), None, A.is_equal, None, ["PRI", "c0"], ["LFb"])
+    mm(T.B7[:, 0:128], T.LT1[:], T.LF[:, 0:128], True, True, ["LT1", "LFa"], ["B7"])
+    mm(T.B7[:, 128:256], T.LT2[:], T.LF[:, 128:256], True, True, ["LT2", "LFb"], ["B7"])
+    ts(T.HI[:], T.NMI[:], 6, None, A.arith_shift_right, None, ["NMI"], ["HI"])
+    ts(T.LO[:], T.NMI[:], 63, None, A.bitwise_and, None, ["NMI"], ["LO"])
+    cp(T.HIB[:], T.HI[:], ["HI"], ["HIB"])
+    cp(T.LOB[:], T.LO[:], ["LO"], ["LOB"])
+    dma("S", T.NZ[0:128:16, :], T.HIB[:], ["HIB"], ["NZ"], "nz")
+    dma("S", T.NZ[1:128:16, :], T.LOB[:], ["LOB"], ["NZ"], "nz")
+    tt(T.MM[:], T.B7[:, 0:256], T.LF[:], A.mult, ["B7", "LFa", "LFb"], ["MM"])
+    ts(T.Q[:], T.J[:], col(4), -8192.0, A.is_equal, A.mult, ["J", "c4"], ["Q"])
+    tt(T.W16[:], T.MM[:, 0:128], T.MM[:, 128:256], A.add, ["MM"], ["W16"])
+    ts(col(5), col(0), 0.0, 63.0, A.is_equal, A.mult, ["c0"], ["c5"])
+    ts(T.WK[:], T.W16[:], col(0), None, A.add, None, ["W16", "c0"], ["WK"])
+    tt(T.WP[:], T.W16[:], T.PRI[:], A.add, ["W16", "PRI"], ["WP"])
+    act(W1[0][:, 0:128], T.Z0[:], AF.Identity, ["Z0"], ["z0_0"], bias=129.0)
+    for h in range(2):
+        mm(T["B%d" % h][:, 0:64], T.IF2[:], T.PN1[:, 64 * h:64 * h + 64], True, False, ["IF2", "PN1"], ["B%d" % h])
+        mm(T["B%d" % (2 + h)][:, 0:64], T.IF2[:], T.PN2[:, 0:64], True, False, ["IF2", "PN2"], ["B%d" % (2 + h)])
+    for h in range(2):
+        for s in range(8 * h, 8 * h + 8):
+            j = s + 1 if s < 7 else s - 6
+            src = "WP" if 7 <= s < 14 else "WK"
+            ts(T.CL[:, 128 * s:128 * s + 128], T[src][:], 16.0 * j, 16.0 * j + 16.0, A.max, A.min, [src], ["CL%d" % h])
+        fold("B%d" % h, 64, T.Q, T.CL, 1024 * h, ["Q", "CL%d" % h], False)
+    ts(col(9), col(0), 2.0, None, A.is_lt, None, ["c0"], ["c9"])
+    ts(T.IA[:], T.J[:, 0:128], 0.0, -1.0 / 32, A.is_equal, A.mult, ["J"], ["IA"])
+    tt(col(5), col(5), col(9), A.add, ["c5", "c9"], ["c5"])
+    ts(T.LFE[:, 0:8], T.J[:, 0:8], 0.0, col(2), A.mult, A.add, ["J", "c0"], ["LFE"])
+    ts(T.Q2[:], T.J[:], col(4), col(5), A.is_equal, A.mult, ["J", "c4", "c5"], ["Q2"])
+    for h in range(2):
+        bank, on, o = "B%d" % h, "ON%d" % h, 64 * h
+        ts(T.ON[:, o:o + 64], T[bank][:, 0:64], -1.0 / 64, col(0), A.mult, A.add, [bank, "c0"], [on])
+        act(T.CL[:, 16 * o:16 * o + 512], T.NZ[:].indirect(T.ON[:, o:o + 32]), AF.Copy, ["NZ", on], ["CL%ds" % h])
+        cp(T.CL[:, 16 * o + 512:16 * o + 1024], T.NZ[:].indirect(T.ON[:, o + 32:o + 64]), ["NZ", on], ["CL%dv" % h])
+        act(T.RN[:, o:o + 64], T[bank][:, 0:64], AF.Identity, [bank], ["RN%d" % h], scale=-1.0)
+        if h == 0:
+            ts(T.IB[:], T.J[:, 0:128], 0.0, -1.0 / 16, A.is_equal, A.mult, ["J"], ["IB"])
+            ms(T.A63[:], 0.0, ["A63"])
+    for h in range(2):
+        fold("B%d" % (2 + h), 64, T.Q2, T.CL, 1024 * h, ["Q2", "CL%ds" % h, "CL%dv" % h], False)
+    tt(T.RP[:], T.RN[:], T.PN3[:], A.subtract, ["RN0", "RN1", "PN3"], ["RP"])
+    ts(T.JJ[:], T.JJ[:], col(0), None, A.add, None, ["JJ", "c0"], ["JJ"])
+    ts(col(6), col(2), 14.0, col(3), A.mult, A.add, ["c0"], ["c6"])
+    ts(T.QI[:], T.JJ[:], -6.5, 1.0 / 14, A.add, A.mult, ["JJ"], ["QI"])
+    ts(col(8), col(0), 32.0, None, A.mult, None, ["c0"], ["c8"])
+    ts(T.QW[:], T.QI[:], 3, None, A.arith_shift_right, None, ["QI"], ["QW"])
+    ts(T.QF[:], T.QI[:], -111.0, None, A.mult, None, ["QI"], ["QF"])
+    ts(T.JJ[:], T.JJ[:], 8.0, None, A.mult, None, ["JJ", "QI"], ["JJ"])
+    cp(T.LC[:], T.QI[:], ["QI"], ["LC"])
+    ts(T.QG[:], T.QW[:], 104.0, None, A.mult, None, ["QW"], ["QG"])
+    tt(T.QF[:], T.QF[:], T.JJ[:], A.add, ["QF", "JJ"], ["QF"])
+    ts(T.L12[:, 0:7], T.C2[:, 0:7], col(6), None, A.add, None, ["C2", "c6"], ["L12a"])
+    tt(T.QF[:], T.QF[:], T.QG[:], A.add, ["QF", "QG"], ["QF"])
+    ts(T.L12[:, 8:15], T.C2[:, 0:7], col(6), 112.0, A.add, A.add, ["C2", "c6"], ["L12c"])
+    ts(T.CB[:], T.C512[:], col(8), None, A.add, None, ["C512", "c8"], ["CB"])
+    cp(T.LTP[:], T.QF[:], ["QF"], ["LTP"])
+    ts(T.TH[:, 0:TS], T.THI[:, 0:TS], 8192.0, 256.0, A.mult, A.add, ["THI"], ["TH"])
+    for h in range(2):
+        cp(T.WA[:, 64 * h:64 * h + 64], T["B%d" % (2 + h)][:, 0:64], ["B%d" % (2 + h)], ["WA"])
+
+    def offers(buf, o, key):
+        tt(T.TT[:, 0:112], buf[:, o + 112:o + 120].indirect(T.LFE[:, 0:7]), buf[:, o:o + 112], A.subtract, [key, "LFE"], ["TTa"])
+        tt(T.TT[:, 112:224], buf[:, o + 120:o + 128].indirect(T.LFE[:, 0:7]), buf[:, o:o + 112], A.subtract, [key, "LFE"], ["TTb"])
+
+    def update(t, buf, o, key):
+        n, sk = 128 * t, "SL%d" % t
+        tt(T.MK[:], T.CI[:, 16 * t:16 * t + 16].indirect(T.LC[:, 0:14]), T.PAT[:], A.is_equal, ["CI%d" % t, "LC", "PAT"], ["MK"])
+        tt(T.DW[:, 0:224], T.TT[:].indirect(T.LTP[:, 0:14]), T.MK[:], A.mult, ["TTa", "TTb", "LTP", "MK"], ["DWd"])
+        tt(T.SL[:, n:n + 112], T.DW[:, 0:224].indirect(T.L12[:, 8:15]), buf[:, o:o + 112], A.add, ["DWd", "L12c", key], [sk + "a"])
+        if t < TS:
+            taken(224)
+        tt(T.SL[:, n:n + 112], T.DW[:, 0:224].indirect(T.L12[:, 0:7]), T.SL[:, n:n + 112], A.add, ["DWd", "L12a", sk + "a"], [sk + "a"])
+        if t < TS:
+            tt(T.SL[:, n + 112:n + 120], T.DW[:, 237:349:14], buf[:, o + 112:o + 120], A.add, ["DWs", key], [sk + "b"])
+            tt(T.SL[:, n + 120:n + 128], T.DW[:, 349:448:14], buf[:, o + 120:o + 128], A.add, ["DWs", key], [sk + "b"])
+
+    def taken(n):
+        op("V", lambda: g.vector.tensor_tensor_scan(T.DW[:, 224:224 + n], T.RST[:, 0:n], T.DW[:, 0:n], 0.0, A.mult, A.subtract), ["RST", "DWd"], ["DWs"])
+
+    xc = [(0, 512), (512, 896), (896, 1408), (1408, 1792)]
+    yc = [(0, 512), (512, 896), (896, 1408), (1408, 1664), (1664, 1792)]
+    for t in range(TS):
+        w1, S, zn, co = W1[t], T.SL[:, 128 * t:128 * t + 128], T["ZN_%d" % t], 16 * t
+        sk, z1, z4, z16 = ["SL%da" % t, "SL%db" % t], "z0_%d" % t, "z4_%d" % t, "z16_%d" % t
+        act(w1[:, 128:256], w1[:, 0:128], AF.Copy, [z1], [z1 + "b"])
+        act(w1[:, 256:512], w1[:, 0:256], AF.Copy, [z1, z1 + "b"], [z4])
+        for k in range(1, 4):
+            dma("Y", w1[:, 512 * k:512 * k + 512], w1[:, 0:512], [z1, z1 + "b", z4], [z16], z16)
+        if t > 0:
+            ts(T.RP[:], S, MAGIC, MAGIC, A.add, A.subtract, sk, ["RP"])
+            send(t, "s", T.PL[:, 128 * t + 128:128 * t + 256], S, sk)
+            tt(T.WA[:], S, T.RP[:], A.subtract, sk + ["RP"], ["WA"])
+        ts(T.BL[:, 0:56], T.WA[:, 56:112], 3232.0, None, A.add, None, ["WA"], ["BL"])
+        ts(T.BL[:, 56:112], T.WA[:, 0:56], 3232.0, None, A.add, None, ["WA"], ["BL"])
+        act(T.B4[:, 0:56], T.WA[:, 56:112], AF.Identity, ["WA", "A63"], ["B4"], bias=T.A63[:, 0:1], scale=2400.0)
+        act(T.B4[:, 56:112], T.WA[:, 0:56], AF.Identity, ["WA", "A63"], ["B4"], bias=T.A63[:, 0:1], scale=2400.0)
+        hx, hy = T.HP[:, 0:112], T.HP[:, 112:224]
+        tt(hy, T.WA[:, 112:120].indirect(T.LFE[:, 0:7]), T.BL[:], A.mult, ["WA", "BL", "LFE"], ["hy"])
+        tt(hx, T.WA[:, 0:112], T.BL[:], A.mult, ["WA", "BL"], ["hx"])
+        for h, k in ((hy, "hy"), (hx, "hx")):
+            tt(h, h, T.B4[:, 0:112], A.add, [k, "B4"], [k])
+        for h, k in ((hy, "hy"), (hx, "hx")):
+            ts(h, h, 5, 4095, A.arith_shift_right, A.bitwise_and, [k], [k])
+        if t == 0:
+            tt(S, T.WA[:], T.RP[:], A.add, ["WA", "RP"], sk)
+            send(t, "s", T.PL[:, 128:256], S, sk)
+        cp(T.OFF[:, 0:112], hx, ["hx"], ["ox"])
+        cp(T.OFF[:, 112:224], hy, ["hy"], ["oy"])
+        zr = [z1, z1 + "b", z4]
+        for bank, ii, r0, pat, p0 in (("B0", "IA", 0, "PTX", 0), ("B1", "IA", 56, "PTX", 56), ("B2", "IB", 56, "PTY", 0), ("B3", "IB", 0, "PTY", 56)):
+            mm(T[bank][:, 0:56], T.ID[:], T[pat][:, p0:p0 + 56], True, False, ["ID", pat], [bank])
+            mm(T[bank][:, 0:56], T[ii][:], T.RP[:, r0:r0 + 56], False, False, [ii, "RP"], [bank])
+        for n, (a, b) in enumerate(xc):
+            tt(T.DX[:, a:b], T.X[:].indirect(T.OFF[:, a // 16:b // 16]), w1[:, 0:b - a], A.subtract, ["X", "ox"] + zr, ["dx%d" % n])
+            act(w1[:, 2048 + a:2048 + b], T.DX[:, a:b], AF.Abs, ["dx%d" % n], ["ax%d_%d" % (n, t)], bias=129.0)
+            if n % 2 == 1:
+                fold("B%d" % (n // 2), 56, T.Q, w1, 2048 + 896 * (n // 2), ["Q", "ax%d_%d" % (n - 1, t), "ax%d_%d" % (n, t)], False)
+        for n, (a, b) in enumerate(yc):
+            tt(T.W2[:, a:b], T.X[:].indirect(T.OFF[:, 112 + a // 16:112 + b // 16]), w1[:, 0:b - a], A.subtract, ["X", "oy"] + zr, ["dy%d" % n])
+            if n == 0:
+                act(T.K2[:, 56:112], T.B0[:, 0:56], AF.Copy, ["B0"], ["K2b"])
+            act(T.AY[:, a:b], T.W2[:, a:b], AF.Abs, ["dy%d" % n], ["ay%d" % n], bias=129.0)
+            if n == 1:
+                fold("B2", 56, T.Q, T.AY, 0, ["Q", "ay0", "ay1"], False)
+                act(T.K2[:, 0:56], T.B1[:, 0:56], AF.Copy, ["B1"], ["K2a"])
+        fold("B3", 56, T.Q, T.AY, 896, ["Q", "ay2", "ay3", "ay4"], False)
+        for a in range(8):
+            op("V", lambda a=a: g.vector.tensor_reduce(T.M2[:, a:a + 1], T.K2[:, a:112:8], AxisListType.X, A.max), ["K2a", "K2b"], ["M2"])
+        tt(T.K1[:, 0:56], T.B2[:, 0:56], T.K2[:, 0:56], A.subtract, ["B2", "K2a"], ["K1a"])
+        ts(T.M2[:], T.M2[:], 255, None, A.bitwise_and, None, ["M2"], ["M2"])
+        landed(t, "s", "PL%d" % (t + 1))
+        if t < TS - 1:
+            nxt = (T.PL, 128 * t + 128, "PL%d" % (t + 1))
+        else:
+            ts(T.R16[:], T.PL[:, 128 * TS:128 * TS + 128], MAGIC, MAGIC, A.add, A.subtract, ["PL%d" % TS], ["R16"])
+            ts(T.R1[:], T.R16[:], 1.0 / 8192, None, A.mult, None, ["R16"], ["R1"])
+            nxt = (T.R1, 0, "R1")
+        ts(T.K1[:, 112:120], T.M2[:], T.TH[:, t:t + 1], None, A.add, None, ["M2", "TH"], ["K1c"])
+        offers(*nxt)
+        if t == 0:
+            ts(T.DG[:], T.R16S[:], col(0), 4096.0, A.is_equal, A.mult, ["R16S0", "c0"], ["DG"])
+        mm(T.B5[:, 0:128], T.ID[:], T.DG[:], True, False, ["ID", "DG"], ["B5"])
+        tt(T.K1[:, 56:112], T.B3[:, 0:56], T.K2[:, 56:112], A.subtract, ["B3", "K2b"], ["K1b"])
+        for a in range(8):
+            op("V", lambda a=a: g.vector.tensor_reduce(T.MI[:, a:a + 1], T.K1[:, a:120:8], AxisListType.X, A.max), ["K1a", "K1b", "K1c"], ["MI"])
+        c7, c8 = T.CO[:, co:co + 8], T.CO[:, co + 8:co + 16]
+        ts(c8, T.MI[:], 255, None, A.bitwise_and, None, ["MI"], ["C8_%d" % t])
+        ts(c7, T.MI[:], 127, None, A.bitwise_and, None, ["MI"], ["C7_%d" % t])
+        send(t, "c", T.CI[:, co + 16:co + 32], T.CO[:, co:co + 16], ["C7_%d" % t, "C8_%d" % t])
+        ts(T.OZ[:], c8, 16.0, col(0), A.mult, A.add, ["C8_%d" % t, "c0"], ["OZ"])
+        dys = ["dy%d" % n for n in range(5)]
+        axs = ["ax%d_%d" % (n, t) for n in range(4)]
+        act(T.TZ[:], T.W2[:].indirect(T.OZ[:]), AF.Identity, ["OZ", "W2c"] + dys, ["TZ"], bias=64.25, scale=0.5)
+        ts(T.EB[:], c8, 128.0, None, A.is_ge, None, ["C8_%d" % t], ["EB"])
+        if t == 0:
+            ts(T.R16S[:], T.R16S[:], 1.0, None, A.min, None, ["R16S0", "DG"], ["R16S"])
+        mm(T.B6[:, 0:8], T.BO[:], T.EB[:], True, True, ["BO", "EB"], ["B6"])
+        act(T.EJ[:], T.B6[:, 0:8], AF.Identity, ["B6"], ["EJ", "YE%d" % t], acc=T.YE[:, t:t + 1])
+        tt(zn[:], w1[:].indirect(T.OZ[:]), T.TZ[:], A.add, ["OZ", "TZ", z16] + zr + axs, ["ZN%d" % t])
+        send(t, "z", W1[t + 1][:, 0:128] if t < TS - 1 else T.ZF[:], zn[:], ["ZN%d" % t])
+        mm(T.B5[:, 0:128], T.BO[:], zn[:], False, True, ["BO", "ZN%d" % t], ["B5"])
+        if t < TS - 1:
+            ts(T.AI[:, 0:1], T.YE[:, t:t + 1], 32.0, T.A63[:, 0:1], A.mult, A.add, ["YE%d" % t, "A63"], ["AI"])
+        op("V", lambda: g.vector.tensor_tensor_scan(T.US[:], T.R16S[:], T.B5[:, 0:128], 0.0, A.mult, A.max), ["R16S", "B5"], ["US"])
+        if t < TS - 1:
+            ts(T.AI[:, 0:1], T.AI[:, 0:1], 63 * 32, None, A.bitwise_and, None, ["AI"], ["AI"])
+        ts(T.UI[:], T.US[:, 15:128:16], -2064.0 - 4096.0, None, A.add, None, ["US"], ["UI"])
+        if t < TS - 1:
+            cp(T.A63[:, 0:1], T.AI[:, 0:1], ["AI"], ["A63"])
+        ts(T.UI[:], T.UI[:], 31, None, A.bitwise_and, None, ["UI"], ["UI"])
+        tt(T.UI[:], T.UI[:], T.CB[:], A.add, ["UI", "CB"], ["UI"])
+        cp(T.CU[:], T.UI[:], ["UI"], ["CU"])
+        tt(T.TA[:], T.X[:].indirect(T.CU[:]), zn[:], A.add, ["X", "CU", "ZN%d" % t], ["TA"])
+        ts(T.TA[:], T.TA[:], 0.5, 64.25, A.mult, A.add, ["TA"], ["TA"])
+        if t == 0:
+            ts(T.RST[:], T.RST[:], 1.0, None, A.min, None, ["RST0"], ["RST"])
+        if t == 1:
+            ts(T.IH[:], T.IH[:], col(0), None, A.is_equal, None, ["IH", "c0"], ["IH"])
+        if t == 2:
+            ts(T.IL[:], T.IL[:], col(0), None, A.subtract, None, ["IL", "c0"], ["IL"])
+        tt(T.X[:].indirect(T.CU[:]), T.TA[:], T.M129[:], A.add, ["TA", "CU", "M129"], ["X"])
+        if t == 3:
+            tt(T.ID2[:, 0:256], T.IH[:], T.IL[:], A.mult, ["IH", "IL"], ["ID2a"])
+        if t == TS - 1:
+            dma("Y", T.yx[:, 0:2048], T.X[:, 0:2048], ["X"], ["o1"], "out")
+            dma("Y", T.yx[:, 2048:4096], T.X[:, 2048:4096], ["X"], ["o1"], "out")
+            dma("S", T.ye[:], T.YE[:, 0:TS], ["YE%d" % k for k in range(TS)], ["o2"], "out2")
+        landed(t, "c", "CI%d" % (t + 1))
+        landed(t, "z", "z0_%d" % (t + 1))
+        update(t + 1, *nxt)
+
+    act(T.YZ[:], T.ZF[:], AF.Identity, ["z0_%d" % TS], ["YZ"], bias=-129.0)
+    dma("S", T.yz[:], T.YZ[:], ["YZ"], ["o2"], "out2")
+    n, ka, kb = 128 * TS, "SL%da" % TS, "SL%db" % TS
+    ts(T.R16[:, 0:112], T.SL[:, n:n + 112], 16.0, None, A.mult, None, [ka], ["R16"])
+    tt(T.CC[:, 56:112], T.R16[:, 56:112], T.SL[:, n:n + 56], A.add, ["R16", ka], ["CCb"])
+    tt(T.CC[:, 0:56], T.R16[:, 0:56], T.SL[:, n + 56:n + 112], A.add, ["R16", ka], ["CCa"])
+    idk = ["ID2a", "ID2b"]
+    cp(T.OP[:, 56:112], T.CC[:, 56:112], ["CCb"], ["OPb"])
+    cp(T.OP[:, 0:56], T.CC[:, 0:56], ["CCa"], ["OPa"])
+    taken(112)
+    tt(T.SL[:, n + 112:n + 120], T.DW[:, 237:349:14], T.R1[:, 112:120], A.add, ["DWs", "R1"], [kb])
+    ts(T.OP[:, 128:136], T.SL[:, n + 112:n + 120], 256.0, None, A.add, None, [kb], ["OPf"])
+    parts = [(0, 2), (2, 4), (4, 6), (6, 7)]
+    for n, (a, b) in enumerate(parts):
+        act(T.G2[:, 128 * a:128 * b], T.ID2[:].indirect(T.OP[:, 56 + 8 * a:56 + 8 * b]), AF.Copy, idk + ["OPb"], ["G%d" % n])
+        tt(T.CL[:, 128 * a:128 * b], T.ID2[:].indirect(T.OP[:, 8 * a:8 * b]), T.G2[:, 128 * a:128 * b], A.add,
+           idk + ["OPa", "G%d" % n], ["H%d" % n, "CL0s", "CL0v"])
+        for s in range(a, b):
+            mm(T.B7[:, 0:128], T.ID[:], T.CL[:, 128 * s:128 * s + 128], s == 0, s == 6, ["ID", "H%d" % n], ["B7"])
+    act(T.YF[:], T.ID2[:].indirect(T.OP[:, 128:136]), AF.Copy, idk + ["OPf"], ["YF"])
+    dma("S", T.yf[:], T.YF[0:128:16, :], ["YF"], ["o2"], "out2")
+    ts(T.YP[:], T.B7[:, 0:128], col(0), None, A.add, None, ["B7", "c0"], ["YP"])
+    dma("S", T.yp[:], T.YP[:], ["YP"], ["o2"], "out2")
+
+    dsem, dcount = {}, {}
+    lastw, readers = {}, {}
+    for n, o in enumerate(ops):
+        deps = set()
+        for k in o["r"]:
+            for m in lastw.get(k, []):
+                deps.add(m)
+            if k[0] == "B" and len(k) == 2 and k[1].isdigit():
+                deps.update(m for m in readers.get(k, []) if ops[m]["q"] != o["q"])
+        for k in o["w"]:
+            for m in readers.get(k, []) + lastw.get(k, []):
+                same = ops[m]["q"] == o["q"] and ops[m]["dma"] is None and o["dma"] is None
+                twin = o["dma"] is not None and ops[m]["dma"] == o["dma"]
+                if not same and not twin and ops[m]["dma"] != "remote":
+                    deps.add(m)
+        o["deps"] = deps if o["kind"] == "op" else set()
+        for k in o["r"]:
+            readers.setdefault(k, []).append(n)
+        for k in o["w"]:
+            if readers.get(k) or k not in lastw:
+                lastw[k] = [n]
+                readers[k] = []
+            else:
+                lastw[k] = lastw[k] + [n]
+        if o["dma"] not in (None, "remote"):
+            dsem.setdefault(o["dma"], "d%d" % len(dsem))
+            dcount[o["dma"]] = dcount.get(o["dma"], 0) + 16
+    known = {q: {} for q in Q}
+    for n, o in enumerate(ops):
+        if o["kind"] != "op":
+            o["clock"] = {}
+            continue
+        kn = known[o["q"]]
+        best = {}
+        for m in o["deps"]:
+            d = ops[m]
+            key = d["q"] if d["kind"] == "op" and d["dma"] is None else (d["dma"] if d["kind"] == "op" else d["sem"])
+            best[key] = max(best.get(key, -1), m)
+        o["waits"] = []
+        for key, m in sorted(best.items(), key=lambda e: -e[1]):
+            if kn.get(key, -1) >= m:
+                continue
+            o["waits"].append(m)
+            ops[m]["inc"] = True
+            d = ops[m]
+            if d["kind"] == "op" and d["dma"] is not None:
+                m = max(i for i, e in enumerate(ops) if e["dma"] == d["dma"])
+            kn[key] = m
+            for k2, v in d["clock"].items():
+                kn[k2] = max(kn.get(k2, -1), v)
+        o["clock"] = dict(kn)
+    cnt = {q: 0 for q in Q}
+    for o in ops:
+        if o["kind"] == "op" and o["dma"] is None and o.get("inc"):
+            cnt[o["q"]] += 1
+            o["val"] = cnt[o["q"]]
+    for o in ops:
+        if o["kind"] != "op":
+            continue
+        q = Q[o["q"]]
+        for m in o["waits"]:
+            d = ops[m]
+            if d["kind"] == "ext":
+                q.wait_ge(T.sem[d["sem"]], d["n"])
+            elif d["dma"] is None:
+                q.wait_ge(T.sem["c" + d["q"]], d["val"])
+            else:
+                q.wait_ge(T.sem[dsem[d["dma"]]], dcount[d["dma"]])
+        ins = o["fn"]()
+        if o["dma"] is None:
+            if o.get("inc"):
+                ins.then_inc(T.sem["c" + o["q"]], 1)
+        elif o["dma"] != "remote":
+            ins.then_inc(T.sem[dsem[o["dma"]]], 16)
+    g.wait_ge(T.sem.left, left[0])
+    g.sync.wait_ge(T.sem[dsem["out"]], dcount["out"])
+    g.scalar.wait_ge(T.sem[dsem["out2"]], dcount["out2"])

@@ -1,8 +1,8 @@
-from concourse.bass import DstId, RemoteDMATransfer
-from concourse.mybir import dt, AluOpType, AxisListType, ActivationFunctionType
+from concourse.mybir import AluOpType, AxisListType, ActivationFunctionType
 
 TS, N, HOP = 5, 8, 3
 F32, BF, I32, U16 = "float32", "bfloat16", "int32", "uint16"
+WW = 1920
 
 
 def _sb(n, d):
@@ -10,39 +10,43 @@ def _sb(n, d):
 
 
 SCRATCH = {
-    "X": _sb(4096, BF), "W2": _sb(3840, BF), "DX": _sb(1792, BF), "AY": _sb(1792, BF),
+    "X": _sb(4096, BF), "W2": _sb(2 * WW, BF), "DX": _sb(1792, BF), "AY": _sb(1792, BF), "W1": _sb(2 * TS * WW, BF), "ZN": _sb(128 * TS, BF),
     "NMI": _sb(128, I32), "PRI": _sb(128, I32), "Z0": _sb(128, BF), "THI": _sb(8, I32), "TH": _sb(8, F32),
     "PI": _sb(8, I32), "PJ": _sb(8, I32), "COL": _sb(16, F32), "J": _sb(144, F32), "GI": _sb(128, F32),
     "Q": _sb(144, BF), "Q2": _sb(144, BF), "ID": _sb(128, BF), "IA": _sb(128, BF), "IB": _sb(128, BF), "IF": _sb(128, F32),
-    "BO": _sb(128, BF), "LT1": _sb(128, BF), "LT2": _sb(128, BF), "LTF": _sb(128, F32),
+    "BO": _sb(128, BF), "LT1": _sb(128, BF), "LT2": _sb(128, BF), "LTF": _sb(128, F32), "NI": _sb(128, BF), "IF2": _sb(128, F32),
     "HI": _sb(128, I32), "LO": _sb(128, I32), "HIB": _sb(128, BF), "LOB": _sb(128, BF), "NZ": _sb(2048, BF), "CL": _sb(2048, BF),
-    "LF": _sb(256, BF), "MM": _sb(256, BF), "W16": _sb(128, BF), "WK": _sb(128, BF), "WP": _sb(128, BF), "PB": _sb(128, BF),
-    "PN1": _sb(128, F32), "PN2": _sb(128, F32), "RN": _sb(128, F32), "ON": _sb(128, U16),
-    "PTX": _sb(112, BF), "PTY": _sb(112, BF), "PAT": _sb(224, F32), "RST": _sb(224, F32), "CB": _sb(8, F32),
-    "JJ": _sb(16, F32), "QI": _sb(16, I32), "QW": _sb(16, I32), "QF": _sb(16, F32), "QG": _sb(16, F32), "C2": _sb(8, F32), "C512": _sb(8, F32),
-    "LFE": _sb(16, U16), "LC": _sb(16, U16), "LTP": _sb(16, U16), "L12": _sb(16, U16),
-    "RP": _sb(128, BF), "WA": _sb(128, F32), "BL": _sb(112, F32), "HP": _sb(224, I32), "OFF": _sb(224, U16),
-    "K2": _sb(112, F32), "K1": _sb(120, F32), "MI": _sb(8, I32), "M2": _sb(8, I32), "C": _sb(16, I32), "OZ": _sb(8, U16),
-    "TT": _sb(224, F32), "MK": _sb(224, F32), "DW": _sb(448, F32), "TZ": _sb(128, F32),
+    "LF": _sb(256, BF), "MM": _sb(256, BF), "W16": _sb(128, BF), "WK": _sb(128, BF), "WP": _sb(128, BF),
+    "PN1": _sb(128, F32), "PN2": _sb(64, F32), "PN3": _sb(128, F32), "RN": _sb(128, F32), "ON": _sb(128, U16),
+    "PTX": _sb(56, BF), "PTY": _sb(56, BF), "PAT": _sb(112, F32), "RST": _sb(112, F32), "CB": _sb(8, F32),
+    "JJ": _sb(8, F32), "QI": _sb(8, I32), "QW": _sb(8, I32), "QF": _sb(8, F32), "QG": _sb(8, F32), "C2": _sb(8, F32), "C512": _sb(8, F32),
+    "LFE": _sb(8, U16), "LC": _sb(8, U16), "LTP": _sb(8, U16), "L12": _sb(8, U16),
+    "RP": _sb(128, BF), "WA": _sb(128, F32), "BL": _sb(128, F32), "HP": _sb(256, I32), "OFF": _sb(224, U16),
+    "K2": _sb(128, F32), "K1": _sb(128, F32), "MI": _sb(8, I32), "M2": _sb(8, I32), "OZ": _sb(8, U16),
+    "TT": _sb(256, F32), "MK": _sb(224, F32), "DW": _sb(464, F32), "TZ": _sb(128, F32),
     "UI": _sb(8, I32), "CU": _sb(8, U16), "TA": _sb(128, BF), "M129": _sb(128, BF), "EB": _sb(8, BF), "EJ": _sb(8, F32),
     "YE": _sb(8, F32), "AI": _sb(4, I32), "A63": _sb(4, F32),
-    "IH": _sb(256, BF), "IL": _sb(256, BF), "ID2": _sb(272, BF), "R16": _sb(128, F32), "R1": _sb(128, F32), "CC": _sb(128, F32),
+    "IH": _sb(256, BF), "IL": _sb(256, BF), "ID2": _sb(272, BF), "R16": _sb(128, F32), "R1": _sb(136, F32), "CC": _sb(128, F32),
     "OP": _sb(136, U16), "YP": _sb(128, F32), "YF": _sb(128, F32), "YZ": _sb(128, BF), "ZF": _sb(128, BF),
-    "IF2": _sb(128, F32), "PN3": _sb(128, F32), "DG": _sb(128, BF), "R16S": _sb(128, F32), "US": _sb(128, F32), "G2": _sb(896, BF),
+    "DG": _sb(128, BF), "R16S": _sb(128, F32), "US": _sb(128, F32), "G2": _sb(896, BF),
     "SL": _sb(128 * (TS + 1), F32), "PL": _sb(128 * (TS + 1), F32), "CI": _sb(16 * (TS + 1), I32), "CO": _sb(16 * TS, I32),
 }
-for _t in range(TS):
-    SCRATCH["W1_%d" % _t] = _sb(3840, BF)
-    SCRATCH["ZN_%d" % _t] = _sb(128, BF)
 for _t in range(8):
     SCRATCH["B%d" % _t] = ("psum", [128, 512], F32)
 
 SEMAPHORES = (["cV", "cS", "cP", "cG", "left"] + ["d%d" % i for i in range(24)]
-              + ["a%s%d" % (k, i) for k in "zsc" for i in range(TS)])
+              + ["a%s%d" % (k, i) for k in ("z0", "z1", "c0", "c1", "s") for i in range(TS)])
 
 A = AluOpType
 AF = ActivationFunctionType
 MAGIC = float(3 * 2 ** 35)
+FAR, WAKE, SLACK, LEAD = 3.6, 0.15, 0.03, 2.0
+XC = [("B7", 512, 896), ("V", 0, 512)]
+LENGTHS = [("dxs", 0.56), ("dx", 0.72), ("dy0_0", 0.63), ("dy1_0", 0.63), ("dy0_4", 0.46), ("dy1_4", 0.46), ("dy", 0.22), ("ax", 0.47),
+           ("MK", 0.2), ("DWd", 0.2), ("DWs", 0.12), ("SL", 0.13), ("TT", 0.13), ("WA", 0.13), ("Hh", 0.63), ("H", 0.12), ("of", 0.12),
+           ("TA", 0.15), ("X", 0.47), ("US", 0.13), ("ZN", 0.13), ("TZ", 0.15), ("zb", 0.16), ("NZ", 1.06), ("CL0s", 0.73), ("CL0v", 0.72),
+           ("CL1s", 0.73), ("CL1v", 0.72), ("G", 0.65), ("MM", 0.27), ("W16", 0.27), ("WP", 0.27), ("LT", 0.2), ("LF", 0.13), ("ID2a", 0.53),
+           ("I", 0.13), ("Q2", 0.15), ("BO", 0.13), ("LO", 0.13), ("YF", 0.23), ("YZ", 0.13), ("R1", 0.13), ("DG", 0.13), ("NI", 0.13)]
 
 
 def rank_program(g, core, T, topo):
@@ -51,12 +55,37 @@ def rank_program(g, core, T, topo):
         return
     Q = {"V": g.vector, "S": g.scalar, "P": g.tensor, "G": g, "Y": g.sync}
     ops = []
+    sink = [ops]
 
     def op(q, fn, r=(), w=(), dma=None):
-        ops.append({"q": q, "fn": fn, "r": list(r), "w": list(w), "dma": dma, "kind": "op"})
+        sink[0].append({"q": q, "fn": fn, "r": list(r), "w": list(w), "dma": dma, "kind": "op"})
 
-    def arrive(sem, n, w):
-        ops.append({"q": None, "r": [], "w": list(w), "kind": "ext", "sem": sem, "n": n, "dma": None})
+    def ops_n(k, n):
+        for o in sink[0][-k:]:
+            o["cols"] = n
+
+    def chain(fn, *args):
+        sink[0] = []
+        fn(*args)
+        calls, out = sink[0], [[]]
+        sink[0] = ops
+        for c in calls:
+            if c["q"] == "V" and any(d["q"] == "V" for d in out[-1]):
+                out.append([])
+            out[-1].append(c)
+        return out
+
+    def weave(a, b, lead=0, per=1):
+        a, b = list(a), list(b)
+        n = 0
+        while a or b:
+            if a:
+                ops.extend(a.pop(0))
+            n += 1
+            if n > lead or not a:
+                for _ in range(per):
+                    if b:
+                        ops.extend(b.pop(0))
 
     def ts(out, in0, s1, s2, o0, o1, r, w):
         if o1 is None:
@@ -72,6 +101,12 @@ def rank_program(g, core, T, topo):
 
     def ms(out, c, w):
         op("V", lambda: g.vector.memset(out, c), [], w)
+
+    def rmax(out, in_, r, w):
+        op("V", lambda: g.vector.tensor_reduce(out, in_, AxisListType.X, A.max), r, w)
+
+    def scan(out, d0, d1, o1, r, w):
+        op("V", lambda: g.vector.tensor_tensor_scan(out, d0, d1, 0.0, A.mult, o1), r, w)
 
     def act(out, in_, f, r, w, bias=0.0, scale=1.0, acc=None):
         if acc is None:
@@ -91,11 +126,10 @@ def rank_program(g, core, T, topo):
     def dma(q, out, in_, r, w, grp):
         op(q, lambda: Q[q].dma_start(out, in_), r, w, dma=grp)
 
-    def fold(bank, n, sel, data, c0, r, first):
+    def fold(bank, n, sel, data, c0, r):
         for b in range(16):
-            mm(T[bank][:, 0:n], sel[:, 15 - b:143 - b], data[:, c0 + b:c0 + 16 * n:16], first and b == 0, b == 15, r, [bank])
+            mm(T[bank][:, 0:n], sel[:, 15 - b:143 - b], data[:, c0 + b:c0 + 16 * n:16], False, b == 15, r, [bank])
 
-    W1 = [T["W1_%d" % t] for t in range(TS)]
     left = [0]
 
     def send(t, kind, dst, src, r):
@@ -104,47 +138,53 @@ def rank_program(g, core, T, topo):
         mask = topo.mask(core, to)
         left[0] += len(topo.engines(core, to))
         op("G", lambda: g.remote_dma(dst, src, T.sem["a%s%d" % (kind, t)], T.sem.left, pid, rid, mask), r, [], dma="remote")
+        sink[0][-1]["sem"] = "a%s%d" % (kind, t)
 
-    def landed(t, kind, key):
+    for t in range(TS):
         frm = T.cores[(rank - (HOP if t < TS - 1 else -HOP * (TS - 1))) % N]
-        arrive("a%s%d" % (kind, t), len(topo.engines(frm, core)), [key])
+        for kind, key in (("s", "PL%d"), ("c0", "CI0_%d"), ("c1", "CI1_%d"), ("z0", "za0_%d"), ("z1", "za1_%d")):
+            ops.append({"q": None, "r": [], "w": [key % (t + 1)], "kind": "ext", "sem": "a%s%d" % (kind, t),
+                        "n": len(topo.engines(frm, core)), "dma": None})
 
     col = lambda j: T.COL[:, j:j + 1]
 
     dma("Y", T.PRI[:], T.pr[:], [], ["PRI"], "pr")
     dma("S", T.NMI[:], T.nm[:], [], ["NMI"], "nm")
-    dma("S", T.Z0[:], T.z0[:], [], ["Z0"], "z0")
-    dma("S", T.THI[:, 0:TS], T.th[:], [], ["THI"], "th")
     dma("Y", T.X[:, 0:2048], T.xt[:, 0:2048], [], ["X"], "x")
-    dma("Y", T.X[:, 2048:4096], T.xt[:, 2048:4096], [], ["X"], "x")
 
     iota(T.PI[:, 0:1], [[0, 1]], 0, 1, ["PI"], True)
     iota(T.J[:], [[1, 144]], 0, -1, ["J"])
     iota(T.GI[:], [[1, 8], [0, 16]], 0, 0, ["GI"])
-    iota(T.PN1[:, 0:112], [[0, 2], [1920, 7], [-1, 8]], 3072, 0, ["PN1"])
-    iota(T.PN1[:, 112:128], [[1920, 2], [-1, 8]], 1920 * 8 + 1152, 0, ["PN1"])
-    iota(T.PN2[:, 0:64], [[0, 64]], -2, 0, ["PN2"])
-    iota(T.PN3[:], [[0, 16], [1024, 8]], 0, 0, ["PN3"])
-    iota(T.JJ[:], [[16, 16]], 0, 0, ["JJ"])
-    iota(T.C2[:], [[2, 8]], 0, 0, ["C2"])
+    for h in range(2):
+        iota(T.PN1[:, 64 * h:64 * h + 56], [[0, 2], [1920, 7], [-1, 4]], 3072 - 4 * h, 0, ["PN1"])
+        iota(T.PN1[:, 64 * h + 56:64 * h + 64], [[1920, 2], [-1, 4]], 1920 * 8 + 1152 - 4 * h, 0, ["PN1"])
+    iota(T.PN2[:], [[0, 64]], -2, 0, ["PN2"])
+    iota(T.PN3[:], [[4096, 2], [0, 16], [1024, 4]], 0, 0, ["PN3"])
+    iota(T.JJ[:], [[16, 8]], 0, 0, ["JJ"])
+    iota(T.C2[:], [[4, 8]], 0, 0, ["C2"])
     iota(T.C512[:], [[512, 8]], 0, 0, ["C512"])
-    iota(T.PTX[:], [[8, 14], [1, 8]], 128, 0, ["PTX"])
-    iota(T.PTY[:], [[0, 2], [16, 7], [2, 8]], 184, 0, ["PTY"])
-    iota(T.PAT[:, 0:112], [[1, 8], [8, 14]], 0, 0, ["PAT"])
-    iota(T.PAT[:, 112:224], [[1, 8], [-56, 2], [8, 7]], 184, 0, ["PAT"])
-    iota(T.RST[:], [[0, 16], [1, 14]], 0, 0, ["RST0"])
+    iota(T.PTX[:], [[1, 56]], 64, 0, ["PTX"])
+    iota(T.PTY[:], [[0, 2], [8, 7], [2, 4]], 92, 0, ["PTY"])
+    iota(T.BL[:], [[0, 128]], 0, 0, ["BL0", "BL1"])
+    iota(T.PAT[:, 0:56], [[1, 4], [4, 14]], 0, 0, ["PAT"])
+    iota(T.PAT[:, 56:112], [[1, 4], [-28, 2], [4, 7]], 92, 0, ["PAT"])
+    iota(T.RST[:], [[0, 8], [1, 14]], 0, 0, ["RST0"])
+    iota(T.R16S[:], [[0, 8], [1, 16]], 0, 0, ["R16S0"])
+    iota(T.M129[:], [[0, 128]], -129, 0, ["M129"])
+    iota(T.PL[:, 120:128], [[0, 8]], 0, 0, ["pad"])
+    iota(T.R1[:, 0:8], [[0, 8]], 0, 0, ["pad"])
+    for h in range(2):
+        iota(T.DW[:, 232 * h + 112:232 * h + 120], [[0, 8]], 0, 0, ["DWz"])
+        iota(T.W2[:, WW * h + 896:WW * h + WW], [[0, 1024]], 129, 0, ["W2c%d" % h])
     iota(T.IH[:], [[1, 16], [0, 16]], 0, 0, ["IH"])
     iota(T.IL[:], [[0, 16], [1, 16]], 0, 0, ["IL"])
     iota(T.ID2[:, 256:272], [[1, 16]], 0, 0, ["ID2b"])
-    iota(T.R16S[:], [[0, 8], [1, 16]], 0, 0, ["R16S0"])
-    iota(T.M129[:], [[0, 128]], -129, 0, ["M129"])
-    iota(T.W2[:, 1792:3840], [[0, 2048]], 129, 0, ["W2c"])
 
     ms(T.NZ[:], 0.0, ["NZ"])
     ts(T.PJ[:, 0:1], T.PI[:, 0:1], 15, None, A.bitwise_and, None, ["PI"], ["PJ0"])
     ts(T.PJ[:, 1:2], T.PI[:, 0:1], 4, None, A.arith_shift_right, None, ["PI"], ["PJ1"])
-    ts(T.PJ[:, 2:3], T.PI[:, 0:1], 7, None, A.bitwise_and, None, ["PI"], ["PJ2"])
-    ts(T.PJ[:, 3:4], T.PI[:, 0:1], 3, 1, A.arith_shift_right, A.bitwise_and, ["PI"], ["PJ3"])
+    ts(T.PJ[:, 2:3], T.PI[:, 0:1], 3, None, A.bitwise_and, None, ["PI"], ["PJ2"])
+    ts(T.PJ[:, 3:4], T.PI[:, 0:1], 2, 3, A.arith_shift_right, A.bitwise_and, ["PI"], ["PJ3"])
     cp(T.COL[:, 0:4], T.PJ[:, 0:4], ["PJ0", "PJ1", "PJ2", "PJ3"], ["c0"])
     ts(T.LTF[:], T.J[:, 0:128], 0.0, 16.0, A.is_ge, A.mult, ["J"], ["LTF"])
     ts(T.ID[:], T.J[:, 0:128], 0.0, None, A.is_equal, None, ["J"], ["ID"])
@@ -165,217 +205,271 @@ def rank_program(g, core, T, topo):
     cp(T.LOB[:], T.LO[:], ["LO"], ["LOB"])
     dma("S", T.NZ[0:128:16, :], T.HIB[:], ["HIB"], ["NZ"], "nz")
     dma("S", T.NZ[1:128:16, :], T.LOB[:], ["LOB"], ["NZ"], "nz")
+    dma("S", T.Z0[:], T.z0[:], [], ["Z0"], "z0")
+    dma("S", T.X[:, 2048:4096], T.xt[:, 2048:4096], [], ["X"], "x")
+    dma("S", T.THI[:, 0:TS], T.th[:], [], ["THI"], "th")
     tt(T.MM[:], T.B7[:, 0:256], T.LF[:], A.mult, ["B7", "LFa", "LFb"], ["MM"])
     ts(T.Q[:], T.J[:], col(4), -8192.0, A.is_equal, A.mult, ["J", "c4"], ["Q"])
     tt(T.W16[:], T.MM[:, 0:128], T.MM[:, 128:256], A.add, ["MM"], ["W16"])
     ts(col(5), col(0), 0.0, 63.0, A.is_equal, A.mult, ["c0"], ["c5"])
     ts(T.WK[:], T.W16[:], col(0), None, A.add, None, ["W16", "c0"], ["WK"])
     tt(T.WP[:], T.W16[:], T.PRI[:], A.add, ["W16", "PRI"], ["WP"])
-    act(W1[0][:, 0:128], T.Z0[:], AF.Identity, ["Z0"], ["z0_0"], bias=129.0)
     for h in range(2):
-        mm(T["B%d" % h][:, 0:64], T.IF2[:], T.PN1[:, 64 * h:64 * h + 64], True, False, ["IF2", "PN1"], ["B%d" % h])
-        mm(T["B%d" % (2 + h)][:, 0:64], T.IF2[:], T.PN2[:, 0:64], True, False, ["IF2", "PN2"], ["B%d" % (2 + h)])
+        mm(T["B%d" % (2 * h)][:, 0:64], T.IF2[:], T.PN1[:, 64 * h:64 * h + 64], True, False, ["IF2", "PN1"], ["B%d" % (2 * h)])
+        mm(T["B%d" % (2 * h + 1)][:, 0:64], T.IF2[:], T.PN2[:], True, False, ["IF2", "PN2"], ["B%d" % (2 * h + 1)])
     for h in range(2):
-        for s in range(8 * h, 8 * h + 8):
+        for s in range(16):
             j = s + 1 if s < 7 else s - 6
             src = "WP" if 7 <= s < 14 else "WK"
-            ts(T.CL[:, 128 * s:128 * s + 128], T[src][:], 16.0 * j, 16.0 * j + 16.0, A.max, A.min, [src], ["CL%d" % h])
-        fold("B%d" % h, 64, T.Q, T.CL, 1024 * h, ["Q", "CL%d" % h], False)
+            o = 1024 * h + 64 * s
+            ts(T.CL[:, o:o + 64], T[src][:, 64 * h:64 * h + 64], 16.0 * j, 16.0 * j + 16.0, A.max, A.min, [src], ["CL%d" % h])
+        fold("B%d" % (2 * h), 64, T.Q, T.CL, 1024 * h, ["Q", "CL%d" % h])
     ts(col(9), col(0), 2.0, None, A.is_lt, None, ["c0"], ["c9"])
-    ts(T.IA[:], T.J[:, 0:128], 0.0, -1.0 / 32, A.is_equal, A.mult, ["J"], ["IA"])
+    ts(T.LFE[:, 0:4], T.J[:, 0:4], 0.0, col(2), A.mult, A.add, ["J", "c0"], ["LFE"])
     tt(col(5), col(5), col(9), A.add, ["c5", "c9"], ["c5"])
-    ts(T.LFE[:, 0:8], T.J[:, 0:8], 0.0, col(2), A.mult, A.add, ["J", "c0"], ["LFE"])
+    ts(T.LFE[:, 4:8], T.GI[:, 64:68], col(2), None, A.add, None, ["GI", "c0"], ["LFE"])
     ts(T.Q2[:], T.J[:], col(4), col(5), A.is_equal, A.mult, ["J", "c4", "c5"], ["Q2"])
     for h in range(2):
-        bank, on, o = "B%d" % h, "ON%d" % h, 64 * h
+        bank, on, o = "B%d" % (2 * h), "ON%d" % h, 64 * h
         ts(T.ON[:, o:o + 64], T[bank][:, 0:64], -1.0 / 64, col(0), A.mult, A.add, [bank, "c0"], [on])
         act(T.CL[:, 16 * o:16 * o + 512], T.NZ[:].indirect(T.ON[:, o:o + 32]), AF.Copy, ["NZ", on], ["CL%ds" % h])
         cp(T.CL[:, 16 * o + 512:16 * o + 1024], T.NZ[:].indirect(T.ON[:, o + 32:o + 64]), ["NZ", on], ["CL%dv" % h])
         act(T.RN[:, o:o + 64], T[bank][:, 0:64], AF.Identity, [bank], ["RN%d" % h], scale=-1.0)
-        if h == 0:
-            ts(T.IB[:], T.J[:, 0:128], 0.0, -1.0 / 16, A.is_equal, A.mult, ["J"], ["IB"])
-            ms(T.A63[:], 0.0, ["A63"])
+        fold("B%d" % (2 * h + 1), 64, T.Q2, T.CL, 1024 * h, ["Q2", "CL%ds" % h, "CL%dv" % h])
     for h in range(2):
-        fold("B%d" % (2 + h), 64, T.Q2, T.CL, 1024 * h, ["Q2", "CL%ds" % h, "CL%dv" % h], False)
-    tt(T.RP[:], T.RN[:], T.PN3[:], A.subtract, ["RN0", "RN1", "PN3"], ["RP"])
-    ts(T.JJ[:], T.JJ[:], col(0), None, A.add, None, ["JJ", "c0"], ["JJ"])
-    ts(col(6), col(2), 14.0, col(3), A.mult, A.add, ["c0"], ["c6"])
-    ts(T.QI[:], T.JJ[:], -6.5, 1.0 / 14, A.add, A.mult, ["JJ"], ["QI"])
-    ts(col(8), col(0), 32.0, None, A.mult, None, ["c0"], ["c8"])
-    ts(T.QW[:], T.QI[:], 3, None, A.arith_shift_right, None, ["QI"], ["QW"])
-    ts(T.QF[:], T.QI[:], -111.0, None, A.mult, None, ["QI"], ["QF"])
-    ts(T.JJ[:], T.JJ[:], 8.0, None, A.mult, None, ["JJ", "QI"], ["JJ"])
-    cp(T.LC[:], T.QI[:], ["QI"], ["LC"])
-    ts(T.QG[:], T.QW[:], 104.0, None, A.mult, None, ["QW"], ["QG"])
-    tt(T.QF[:], T.QF[:], T.JJ[:], A.add, ["QF", "JJ"], ["QF"])
-    ts(T.L12[:, 0:7], T.C2[:, 0:7], col(6), None, A.add, None, ["C2", "c6"], ["L12a"])
-    tt(T.QF[:], T.QF[:], T.QG[:], A.add, ["QF", "QG"], ["QF"])
-    ts(T.L12[:, 8:15], T.C2[:, 0:7], col(6), 112.0, A.add, A.add, ["C2", "c6"], ["L12c"])
-    ts(T.CB[:], T.C512[:], col(8), None, A.add, None, ["C512", "c8"], ["CB"])
-    cp(T.LTP[:], T.QF[:], ["QF"], ["LTP"])
-    ts(T.TH[:, 0:TS], T.THI[:, 0:TS], 8192.0, 256.0, A.mult, A.add, ["THI"], ["TH"])
-    for h in range(2):
-        cp(T.WA[:, 64 * h:64 * h + 64], T["B%d" % (2 + h)][:, 0:64], ["B%d" % (2 + h)], ["WA"])
+        act(T.W1[:, WW * h:WW * h + 64], T.Z0[:, 64 * h:64 * h + 64], AF.Identity, ["Z0"], ["za%d_0" % h], bias=129.0)
+    ts(T.IA[:], T.J[:, 0:128], 0.0, -1.0 / 32, A.is_equal, A.mult, ["J"], ["IA"])
+    ts(T.IB[:], T.J[:, 0:128], 0.0, -1.0 / 16, A.is_equal, A.mult, ["J"], ["IB"])
+    ms(T.A63[:], 0.0, ["A63"])
+    ts(T.NI[:], T.J[:, 0:128], 0.0, -1.0, A.is_equal, A.mult, ["J"], ["NI"])
+    tt(T.RP[:], T.RN[:], T.PN3[:], A.subtract, ["RN0", "RN1", "PN3"], ["RP0", "RP1"])
 
-    def offers(buf, o, key):
-        tt(T.TT[:, 0:112], buf[:, o + 112:o + 120].indirect(T.LFE[:, 0:7]), buf[:, o:o + 112], A.subtract, [key, "LFE"], ["TTa"])
-        tt(T.TT[:, 112:224], buf[:, o + 120:o + 128].indirect(T.LFE[:, 0:7]), buf[:, o:o + 112], A.subtract, [key, "LFE"], ["TTb"])
+    def lists():
+        ts(T.JJ[:], T.JJ[:], col(0), None, A.add, None, ["JJ", "c0"], ["JJ"])
+        ts(col(6), col(2), 14.0, col(3), A.mult, A.add, ["c0"], ["c6"])
+        ts(T.QI[:], T.JJ[:], -6.5, 1.0 / 14, A.add, A.mult, ["JJ"], ["QI"])
+        ts(col(8), col(0), 32.0, None, A.mult, None, ["c0"], ["c8"])
+        ts(T.QW[:], T.QI[:], 2, None, A.arith_shift_right, None, ["QI"], ["QW"])
+        ts(T.QF[:], T.QI[:], -55.0, None, A.mult, None, ["QI"], ["QF"])
+        ts(T.JJ[:], T.JJ[:], 4.0, None, A.mult, None, ["JJ", "QI"], ["JJ"])
+        cp(T.LC[:], T.QI[:], ["QI"], ["LC"])
+        ts(T.QG[:], T.QW[:], 60.0, None, A.mult, None, ["QW"], ["QG"])
+        tt(T.QF[:], T.QF[:], T.JJ[:], A.add, ["QF", "JJ"], ["QF"])
+        ts(T.L12[:, 0:3], T.C2[:, 0:3], col(6), None, A.add, None, ["C2", "c6"], ["L12"])
+        tt(T.QF[:], T.QF[:], T.QG[:], A.add, ["QF", "QG"], ["QF"])
+        ts(T.L12[:, 4:7], T.C2[:, 0:3], col(6), 56.0, A.add, A.add, ["C2", "c6"], ["L12"])
+        ts(T.CB[:], T.C512[:], col(8), None, A.add, None, ["C512", "c8"], ["CB"])
+        cp(T.LTP[:], T.QF[:], ["QF"], ["LTP"])
+        ts(col(10), col(3), 2.0, 119.0, A.is_ge, A.mult, ["c0"], ["c10"])
+        ts(col(11), col(3), 3.0, 55.0, A.is_ge, A.mult, ["c0"], ["c11"])
+        ts(col(12), col(6), -1.0, 44.0, A.mult, A.add, ["c6"], ["c12"])
+        ts(col(10), col(10), col(11), 12.0, A.add, A.add, ["c10", "c11"], ["c10"])
+        ts(col(12), col(3), 2.0, col(12), A.is_ge, A.mult, ["c0", "c12"], ["c12"])
+        ts(T.L12[:, 3:4], col(10), col(6), None, A.add, None, ["c10", "c6"], ["L12"])
+        ts(T.L12[:, 7:8], col(12), col(6), 68.0, A.add, A.add, ["c12", "c6"], ["L12"])
+        ts(T.TH[:, 0:TS], T.THI[:, 0:TS], 8192.0, 256.0, A.mult, A.add, ["THI"], ["TH"])
+        ts(T.DG[:], T.R16S[:], col(0), 4096.0, A.is_equal, A.mult, ["R16S0", "c0"], ["DG"])
+        ts(T.RST[:], T.RST[:], 1.0, None, A.min, None, ["RST0"], ["RST"])
+        ts(T.R16S[:], T.R16S[:], 1.0, None, A.min, None, ["R16S0", "DG"], ["R16S"])
 
-    def update(t, buf, o, key):
-        n, sk = 128 * t, "SL%d" % t
-        tt(T.MK[:], T.CI[:, 16 * t:16 * t + 16].indirect(T.LC[:, 0:14]), T.PAT[:], A.is_equal, ["CI%d" % t, "LC", "PAT"], ["MK"])
-        tt(T.DW[:, 0:224], T.TT[:].indirect(T.LTP[:, 0:14]), T.MK[:], A.mult, ["TTa", "TTb", "LTP", "MK"], ["DWd"])
-        tt(T.SL[:, n:n + 112], T.DW[:, 0:224].indirect(T.L12[:, 8:15]), buf[:, o:o + 112], A.add, ["DWd", "L12c", key], [sk + "a"])
-        if t < TS:
-            taken(224)
-        tt(T.SL[:, n:n + 112], T.DW[:, 0:224].indirect(T.L12[:, 0:7]), T.SL[:, n:n + 112], A.add, ["DWd", "L12a", sk + "a"], [sk + "a"])
-        if t < TS:
-            tt(T.SL[:, n + 112:n + 120], T.DW[:, 237:349:14], buf[:, o + 112:o + 120], A.add, ["DWs", key], [sk + "b"])
-            tt(T.SL[:, n + 120:n + 128], T.DW[:, 349:448:14], buf[:, o + 120:o + 128], A.add, ["DWs", key], [sk + "b"])
+    def before(t, h):
+        return (T.PL, 128 * t + 64 * h, "PL%d" % t) if t < TS else (T.R1, 64 * h + 8, "R1")
 
-    def taken(n):
-        op("V", lambda: g.vector.tensor_tensor_scan(T.DW[:, 224:224 + n], T.RST[:, 0:n], T.DW[:, 0:n], 0.0, A.mult, A.subtract), ["RST", "DWd"], ["DWs"])
+    def offers(t, h):
+        buf, o, key = before(t, h)
+        for w in range(2):
+            c = 128 * h + 64 * w
+            tt(T.TT[:, c:c + 64], buf[:, o + 56:o + 64].indirect(T.LFE[:, 4 * w:4 * w + 4]), buf[:, o - 8:o + 56], A.subtract, [key, "LFE", "pad"], ["TT%d" % h])
 
-    xc = [(0, 512), (512, 896), (896, 1408), (1408, 1792)]
-    yc = [(0, 512), (512, 896), (896, 1408), (1408, 1664), (1664, 1792)]
-    for t in range(TS):
-        w1, S, zn, co = W1[t], T.SL[:, 128 * t:128 * t + 128], T["ZN_%d" % t], 16 * t
-        sk, z1, z4, z16 = ["SL%da" % t, "SL%db" % t], "z0_%d" % t, "z4_%d" % t, "z16_%d" % t
-        act(w1[:, 128:256], w1[:, 0:128], AF.Copy, [z1], [z1 + "b"])
-        act(w1[:, 256:512], w1[:, 0:256], AF.Copy, [z1, z1 + "b"], [z4])
-        for k in range(1, 4):
-            dma("Y", w1[:, 512 * k:512 * k + 512], w1[:, 0:512], [z1, z1 + "b", z4], [z16], z16)
+    def update(t, h):
+        buf, o, key = before(t, h)
+        n, sk, d, ci = 128 * t + 64 * h, "SL%d_%d" % (h, t), 232 * h, 16 * t + 8 * h
+        mk, dw = T.MK[:, 112 * h:112 * h + 112], T.DW[:, d:d + 112]
+        tt(mk, T.CI[:, ci:ci + 8].indirect(T.LC[:, 0:7]), T.PAT[:], A.is_equal, ["CI%d_%d" % (h, t), "LC", "PAT"], ["MK%d" % h])
+        tt(dw, T.TT[:, 128 * h + 8:128 * h + 128].indirect(T.LTP[:, 0:7]), mk, A.mult, ["TT%d" % h, "LTP", "MK%d" % h], ["DWd%d" % h])
+        scan(T.DW[:, d + 120:d + 232], T.RST[:], dw, A.subtract, ["RST", "DWd%d" % h], ["DWs%d" % h])
+        tt(T.SL[:, n:n + 64], T.DW[:, d:d + 120].indirect(T.L12[:, 4:8]), buf[:, o:o + 64], A.add, ["DWd%d" % h, "DWz", "L12", key], [sk])
+        tt(T.SL[:, n:n + 64], T.DW[:, d:d + 232].indirect(T.L12[:, 0:4]), T.SL[:, n:n + 64], A.add, ["DWd%d" % h, "DWs%d" % h, "DWz", "L12", sk], [sk])
+
+    def columns(t, h):
+        o, n, sk, w = 64 * h, 128 * t + 64 * h, "SL%d_%d" % (h, t), WW * (2 * t + h)
+        wa, rp, bl, za, z4, z16 = "WA%d" % h, "RP%d" % h, "BL%d" % h, "za%d_%d" % (h, t), "zb%d_%d" % (h, t), "zc%d_%d" % (h, t)
         if t > 0:
-            ts(T.RP[:], S, MAGIC, MAGIC, A.add, A.subtract, sk, ["RP"])
-            send(t, "s", T.PL[:, 128 * t + 128:128 * t + 256], S, sk)
-            tt(T.WA[:], S, T.RP[:], A.subtract, sk + ["RP"], ["WA"])
-        ts(T.BL[:, 0:56], T.WA[:, 56:112], 3232.0, None, A.add, None, ["WA"], ["BL"])
-        ts(T.BL[:, 56:112], T.WA[:, 0:56], 3232.0, None, A.add, None, ["WA"], ["BL"])
-        act(T.B4[:, 0:56], T.WA[:, 56:112], AF.Identity, ["WA", "A63"], ["B4"], bias=T.A63[:, 0:1], scale=2400.0)
-        act(T.B4[:, 56:112], T.WA[:, 0:56], AF.Identity, ["WA", "A63"], ["B4"], bias=T.A63[:, 0:1], scale=2400.0)
-        hx, hy = T.HP[:, 0:112], T.HP[:, 112:224]
-        tt(hy, T.WA[:, 112:120].indirect(T.LFE[:, 0:7]), T.BL[:], A.mult, ["WA", "BL", "LFE"], ["hy"])
-        tt(hx, T.WA[:, 0:112], T.BL[:], A.mult, ["WA", "BL"], ["hx"])
-        for h, k in ((hy, "hy"), (hx, "hx")):
-            tt(h, h, T.B4[:, 0:112], A.add, [k, "B4"], [k])
-        for h, k in ((hy, "hy"), (hx, "hx")):
-            ts(h, h, 5, 4095, A.arith_shift_right, A.bitwise_and, [k], [k])
-        if t == 0:
-            tt(S, T.WA[:], T.RP[:], A.add, ["WA", "RP"], sk)
-            send(t, "s", T.PL[:, 128:256], S, sk)
-        cp(T.OFF[:, 0:112], hx, ["hx"], ["ox"])
-        cp(T.OFF[:, 112:224], hy, ["hy"], ["oy"])
-        zr = [z1, z1 + "b", z4]
-        for bank, ii, r0, pat, p0 in (("B0", "IA", 0, "PTX", 0), ("B1", "IA", 56, "PTX", 56), ("B2", "IB", 56, "PTY", 0), ("B3", "IB", 0, "PTY", 56)):
-            mm(T[bank][:, 0:56], T.ID[:], T[pat][:, p0:p0 + 56], True, False, ["ID", pat], [bank])
-            mm(T[bank][:, 0:56], T[ii][:], T.RP[:, r0:r0 + 56], False, False, [ii, "RP"], [bank])
-        for n, (a, b) in enumerate(xc):
-            tt(T.DX[:, a:b], T.X[:].indirect(T.OFF[:, a // 16:b // 16]), w1[:, 0:b - a], A.subtract, ["X", "ox"] + zr, ["dx%d" % n])
-            act(w1[:, 2048 + a:2048 + b], T.DX[:, a:b], AF.Abs, ["dx%d" % n], ["ax%d_%d" % (n, t)], bias=129.0)
-            if n % 2 == 1:
-                fold("B%d" % (n // 2), 56, T.Q, w1, 2048 + 896 * (n // 2), ["Q", "ax%d_%d" % (n - 1, t), "ax%d_%d" % (n, t)], False)
-        for n, (a, b) in enumerate(yc):
-            tt(T.W2[:, a:b], T.X[:].indirect(T.OFF[:, 112 + a // 16:112 + b // 16]), w1[:, 0:b - a], A.subtract, ["X", "oy"] + zr, ["dy%d" % n])
-            if n == 0:
-                act(T.K2[:, 56:112], T.B0[:, 0:56], AF.Copy, ["B0"], ["K2b"])
-            act(T.AY[:, a:b], T.W2[:, a:b], AF.Abs, ["dy%d" % n], ["ay%d" % n], bias=129.0)
-            if n == 1:
-                fold("B2", 56, T.Q, T.AY, 0, ["Q", "ay0", "ay1"], False)
-                act(T.K2[:, 0:56], T.B1[:, 0:56], AF.Copy, ["B1"], ["K2a"])
-        fold("B3", 56, T.Q, T.AY, 896, ["Q", "ay2", "ay3", "ay4"], False)
-        for a in range(8):
-            op("V", lambda a=a: g.vector.tensor_reduce(T.M2[:, a:a + 1], T.K2[:, a:112:8], AxisListType.X, A.max), ["K2a", "K2b"], ["M2"])
-        tt(T.K1[:, 0:56], T.B2[:, 0:56], T.K2[:, 0:56], A.subtract, ["B2", "K2a"], ["K1a"])
-        ts(T.M2[:], T.M2[:], 255, None, A.bitwise_and, None, ["M2"], ["M2"])
-        landed(t, "s", "PL%d" % (t + 1))
-        if t < TS - 1:
-            nxt = (T.PL, 128 * t + 128, "PL%d" % (t + 1))
+            update(t, h)
+            if h == 1:
+                send(t, "s", T.PL[:, 128 * t + 128:128 * t + 256], T.SL[:, 128 * t:128 * t + 128], ["SL0_%d" % t, sk])
+            ts(T.RP[:, o:o + 64], T.SL[:, n:n + 64], MAGIC, MAGIC, A.add, A.subtract, [sk], [rp])
+        for k in (64, 128, 256):
+            act(T.W1[:, w + k:w + 2 * k], T.W1[:, w:w + k], AF.Copy, [za, z4], [z4])
+        dma("Y", T.W1[:, w + 512:w + 1024], T.W1[:, w:w + 512], [za, z4], [z16], z16)
+        if t > 0:
+            tt(T.WA[:, o:o + 64], T.SL[:, n:n + 64], T.RP[:, o:o + 64], A.subtract, [sk, rp], [wa])
         else:
-            ts(T.R16[:], T.PL[:, 128 * TS:128 * TS + 128], MAGIC, MAGIC, A.add, A.subtract, ["PL%d" % TS], ["R16"])
-            ts(T.R1[:], T.R16[:], 1.0 / 8192, None, A.mult, None, ["R16"], ["R1"])
-            nxt = (T.R1, 0, "R1")
-        ts(T.K1[:, 112:120], T.M2[:], T.TH[:, t:t + 1], None, A.add, None, ["M2", "TH"], ["K1c"])
-        offers(*nxt)
+            cp(T.WA[:, o:o + 64], T["B%d" % (2 * h + 1)][:, 0:64], ["B%d" % (2 * h + 1)], [wa])
+        px, py = "B%d" % (2 * h), "B%d" % (2 * h + 1)
+        mm(T[px][:, 0:56], T.ID[:], T.PTX[:], True, False, ["ID", "PTX"], [px])
+        mm(T[px][:, 0:56], T.IA[:], T.RP[:, o:o + 56], False, False, ["IA", rp], [px])
+        mm(T[py][:, 0:56], T.ID[:], T.PTY[:], True, False, ["ID", "PTY"], [py])
+        mm(T[py][:, 0:28], T.IB[:], T.RP[:, o + 28:o + 56], False, False, ["IB", rp], [py])
+        mm(T[py][:, 28:56], T.IB[:], T.RP[:, o:o + 28], False, False, ["IB", rp], [py])
+        ts(T.BL[:, o:o + 28], T.WA[:, o + 28:o + 56], 3232.0, None, A.add, None, [wa], [bl])
+        for k in (0, 56):
+            act(T.B4[:, k:k + 28], T.WA[:, o + 28:o + 56], AF.Identity, [wa, "A63"], ["B4"], bias=T.A63[:, 0:1], scale=2400.0)
+            act(T.B4[:, k + 28:k + 56], T.WA[:, o:o + 28], AF.Identity, [wa, "A63"], ["B4"], bias=T.A63[:, 0:1], scale=2400.0)
+        ts(T.BL[:, o + 28:o + 56], T.WA[:, o:o + 28], 3232.0, None, A.add, None, [wa], [bl])
+        hp, hk = 128 * h, "H%d" % h
+        tt(T.HP[:, hp + 56:hp + 120], T.WA[:, o + 56:o + 64].indirect(T.LFE[:, 0:4]), T.BL[:, o:o + 64], A.mult, [wa, bl, "LFE"], [hk + "y"])
+        tt(T.HP[:, hp:hp + 56], T.WA[:, o:o + 56], T.BL[:, o:o + 56], A.mult, [wa, bl], [hk])
+        hh = T.HP[:, hp:hp + 112]
+        tt(hh, hh, T.B4[:, 0:112], A.add, [hk, hk + "y", "B4"], [hk])
+        ts(hh, hh, 5, 4095, A.arith_shift_right, A.bitwise_and, [hk], [hk])
+        cp(T.OFF[:, 112 * h:112 * h + 112], hh, [hk], ["of%d" % h])
         if t == 0:
-            ts(T.DG[:], T.R16S[:], col(0), 4096.0, A.is_equal, A.mult, ["R16S0", "c0"], ["DG"])
-        mm(T.B5[:, 0:128], T.ID[:], T.DG[:], True, False, ["ID", "DG"], ["B5"])
-        tt(T.K1[:, 56:112], T.B3[:, 0:56], T.K2[:, 56:112], A.subtract, ["B3", "K2b"], ["K1b"])
-        for a in range(8):
-            op("V", lambda a=a: g.vector.tensor_reduce(T.MI[:, a:a + 1], T.K1[:, a:120:8], AxisListType.X, A.max), ["K1a", "K1b", "K1c"], ["MI"])
-        c7, c8 = T.CO[:, co:co + 8], T.CO[:, co + 8:co + 16]
-        ts(c8, T.MI[:], 255, None, A.bitwise_and, None, ["MI"], ["C8_%d" % t])
-        ts(c7, T.MI[:], 127, None, A.bitwise_and, None, ["MI"], ["C7_%d" % t])
-        send(t, "c", T.CI[:, co + 16:co + 32], T.CO[:, co:co + 16], ["C7_%d" % t, "C8_%d" % t])
-        ts(T.OZ[:], c8, 16.0, col(0), A.mult, A.add, ["C8_%d" % t, "c0"], ["OZ"])
-        dys = ["dy%d" % n for n in range(5)]
-        axs = ["ax%d_%d" % (n, t) for n in range(4)]
-        act(T.TZ[:], T.W2[:].indirect(T.OZ[:]), AF.Identity, ["OZ", "W2c"] + dys, ["TZ"], bias=64.25, scale=0.5)
-        ts(T.EB[:], c8, 128.0, None, A.is_ge, None, ["C8_%d" % t], ["EB"])
-        if t == 0:
-            ts(T.R16S[:], T.R16S[:], 1.0, None, A.min, None, ["R16S0", "DG"], ["R16S"])
-        mm(T.B6[:, 0:8], T.BO[:], T.EB[:], True, True, ["BO", "EB"], ["B6"])
-        act(T.EJ[:], T.B6[:, 0:8], AF.Identity, ["B6"], ["EJ", "YE%d" % t], acc=T.YE[:, t:t + 1])
-        tt(zn[:], w1[:].indirect(T.OZ[:]), T.TZ[:], A.add, ["OZ", "TZ", z16] + zr + axs, ["ZN%d" % t])
-        send(t, "z", W1[t + 1][:, 0:128] if t < TS - 1 else T.ZF[:], zn[:], ["ZN%d" % t])
-        mm(T.B5[:, 0:128], T.BO[:], zn[:], False, True, ["BO", "ZN%d" % t], ["B5"])
+            tt(T.SL[:, o:o + 64], T.WA[:, o:o + 64], T.RP[:, o:o + 64], A.add, [wa, rp], [sk])
+            if h == 1:
+                send(t, "s", T.PL[:, 128:256], T.SL[:, 0:128], ["SL0_0", sk])
+
+    def gathers(t, h):
+        w, d, f, of = WW * (2 * t + h), 896 * h, 112 * h, "of%d" % h
+        zr = ["za%d_%d" % (h, t), "zb%d_%d" % (h, t)]
+        px, py = "B%d" % (2 * h), "B%d" % (2 * h + 1)
+        axs = []
+        for e, a, b in XC:
+            k, ax = "dx%s%d_%d" % (e[0], h, a), "ax%d_%d_%d" % (h, t, a)
+            axs.append(ax)
+            src = T.X[:].indirect(T.OFF[:, f + a // 16:f + b // 16])
+            if e == "V":
+                tt(T.DX[:, d + a:d + b], src, T.W1[:, w:w + b - a], A.subtract, ["X", of] + zr, [k])
+                act(T.W1[:, w + 1024 + a:w + 1024 + b], T.DX[:, d + a:d + b], AF.Abs, [k], [ax], bias=129.0)
+                ops_n(2, b - a)
+            else:
+                act(T.DX[:, d + a:d + b], src, AF.Copy, ["X", of], [k])
+                mm(T[e][:, 0:b - a], T.NI[:], T.W1[:, w:w + b - a], True, False, ["NI"] + zr, [e])
+                mm(T[e][:, 0:b - a], T.ID[:], T.DX[:, d + a:d + b], False, True, ["ID", k], [e])
+                act(T.W1[:, w + 1024 + a:w + 1024 + b], T[e][:, 0:b - a], AF.Abs, [e], [ax], bias=129.0)
+                ops_n(4, b - a)
+        fold(px, 56, T.Q, T.W1, w + 1024, ["Q"] + axs)
+        for a, b in ((0, 448), (448, 768), (768, 896)):
+            k = "dy%d_%d" % (h, a)
+            tt(T.W2[:, WW * h + a:WW * h + b], T.X[:].indirect(T.OFF[:, f + 56 + a // 16:f + 56 + b // 16]), T.W1[:, w:w + b - a], A.subtract, ["X", of] + zr, [k])
+            act(T.AY[:, d + a:d + b], T.W2[:, WW * h + a:WW * h + b], AF.Abs, [k], ["ay%d" % h], bias=129.0)
+        fold(py, 56, T.Q, T.AY, d, ["Q", "ay%d" % h])
+        act(T.K2[:, 64 * h:64 * h + 28], T[px][:, 28:56], AF.Copy, [px], ["K2%d" % h])
+        act(T.K2[:, 64 * h + 28:64 * h + 56], T[px][:, 0:28], AF.Copy, [px], ["K2%d" % h])
+
+    def escape(t, h):
+        o = 64 * h
+        m2 = T.M2[:, 4 * h:4 * h + 4]
+        for a in range(4):
+            rmax(T.M2[:, 4 * h + a:4 * h + a + 1], T.K2[:, o + a:o + 56:4], ["K2%d" % h], ["M2%d" % h])
+        ts(m2, m2, 127, None, A.bitwise_and, None, ["M2%d" % h], ["M2%d" % h])
+        ts(T.K1[:, o + 56:o + 60], m2, T.TH[:, t:t + 1], None, A.add, None, ["M2%d" % h, "TH"], ["K1c%d" % h])
+
+    def choose(t, h):
+        o, w, co, py = 64 * h, WW * (2 * t + h), 16 * t + 8 * h, "B%d" % (2 * h + 1)
+        mi, oz, k7, k8 = T.MI[:, 4 * h:4 * h + 4], T.OZ[:, 4 * h:4 * h + 4], "C7%d_%d" % (h, t), "C8%d_%d" % (h, t)
+        tt(T.K1[:, o:o + 56], T[py][:, 0:56], T.K2[:, o:o + 56], A.subtract, [py, "K2%d" % h], ["K1%d" % h])
+        for a in range(4):
+            rmax(T.MI[:, 4 * h + a:4 * h + a + 1], T.K1[:, o + a:o + 60:4], ["K1%d" % h, "K1c%d" % h], ["MI%d" % h])
+        c7, c8 = T.CO[:, co:co + 4], T.CO[:, co + 4:co + 8]
+        ts(c8, mi, 127, None, A.bitwise_and, None, ["MI%d" % h], [k8])
+        ts(c7, mi, 63, None, A.bitwise_and, None, ["MI%d" % h], [k7])
+        send(t, "c%d" % h, T.CI[:, co + 16:co + 24], T.CO[:, co:co + 8], [k7, k8])
+        ts(oz, c8, 16.0, col(0), A.mult, A.add, [k8, "c0"], ["OZ%d" % h])
+        dys = ["dy%d_%d" % (h, a) for a in (0, 448, 768)]
+        act(T.TZ[:, o:o + 64], T.W2[:, WW * h:WW * h + WW].indirect(oz), AF.Identity, ["OZ%d" % h, "W2c%d" % h] + dys, ["TZ%d" % h], bias=64.25, scale=0.5)
+        ts(T.EB[:, 4 * h:4 * h + 4], c8, 64.0, None, A.is_ge, None, [k8], ["EB%d" % h])
+        if h == 1:
+            mm(T.B5[:, 0:128], T.ID[:], T.DG[:], True, False, ["ID", "DG"], ["B5"])
+            mm(T.B6[:, 0:8], T.BO[:], T.EB[:], True, True, ["BO", "EB0", "EB1"], ["B6"])
+            act(T.EJ[:], T.B6[:, 0:8], AF.Identity, ["B6"], ["EJ", "YE%d" % t], acc=T.YE[:, t:t + 1])
+
+    def newz(t, h):
+        o, w = 64 * h, WW * (2 * t + h)
+        zn, k = T.ZN[:, 128 * t + o:128 * t + o + 64], "ZN%d_%d" % (h, t)
+        tt(zn, T.W1[:, w:w + WW].indirect(T.OZ[:, 4 * h:4 * h + 4]), T.TZ[:, o:o + 64], A.add,
+           ["OZ%d" % h, "TZ%d" % h, "za%d_%d" % (h, t), "zb%d_%d" % (h, t), "zc%d_%d" % (h, t)] + ["ax%d_%d_%d" % (h, t, a) for _, a, _b in XC], [k])
+        send(t, "z%d" % h, T.W1[:, w + 2 * WW:w + 2 * WW + 64] if t < TS - 1 else T.ZF[:, o:o + 64], zn, [k])
+
+    def write(t):
+        zn, zk = T.ZN[:, 128 * t:128 * t + 128], ["ZN0_%d" % t, "ZN1_%d" % t]
+        mm(T.B5[:, 0:128], T.BO[:], zn, False, True, ["BO"] + zk, ["B5"])
         if t < TS - 1:
             ts(T.AI[:, 0:1], T.YE[:, t:t + 1], 32.0, T.A63[:, 0:1], A.mult, A.add, ["YE%d" % t, "A63"], ["AI"])
-        op("V", lambda: g.vector.tensor_tensor_scan(T.US[:], T.R16S[:], T.B5[:, 0:128], 0.0, A.mult, A.max), ["R16S", "B5"], ["US"])
-        if t < TS - 1:
             ts(T.AI[:, 0:1], T.AI[:, 0:1], 63 * 32, None, A.bitwise_and, None, ["AI"], ["AI"])
-        ts(T.UI[:], T.US[:, 15:128:16], -2064.0 - 4096.0, None, A.add, None, ["US"], ["UI"])
-        if t < TS - 1:
             cp(T.A63[:, 0:1], T.AI[:, 0:1], ["AI"], ["A63"])
+        scan(T.US[:], T.R16S[:], T.B5[:, 0:128], A.max, ["R16S", "B5"], ["US"])
+        ts(T.UI[:], T.US[:, 15:128:16], -2064.0 - 4096.0, None, A.add, None, ["US"], ["UI"])
         ts(T.UI[:], T.UI[:], 31, None, A.bitwise_and, None, ["UI"], ["UI"])
         tt(T.UI[:], T.UI[:], T.CB[:], A.add, ["UI", "CB"], ["UI"])
         cp(T.CU[:], T.UI[:], ["UI"], ["CU"])
-        tt(T.TA[:], T.X[:].indirect(T.CU[:]), zn[:], A.add, ["X", "CU", "ZN%d" % t], ["TA"])
+        tt(T.TA[:], T.X[:].indirect(T.CU[:]), zn, A.add, ["X", "CU"] + zk, ["TA"])
         ts(T.TA[:], T.TA[:], 0.5, 64.25, A.mult, A.add, ["TA"], ["TA"])
-        if t == 0:
-            ts(T.RST[:], T.RST[:], 1.0, None, A.min, None, ["RST0"], ["RST"])
-        if t == 1:
-            ts(T.IH[:], T.IH[:], col(0), None, A.is_equal, None, ["IH", "c0"], ["IH"])
-        if t == 2:
-            ts(T.IL[:], T.IL[:], col(0), None, A.subtract, None, ["IL", "c0"], ["IL"])
         tt(T.X[:].indirect(T.CU[:]), T.TA[:], T.M129[:], A.add, ["TA", "CU", "M129"], ["X"])
-        if t == 3:
-            tt(T.ID2[:, 0:256], T.IH[:], T.IL[:], A.mult, ["IH", "IL"], ["ID2a"])
         if t == TS - 1:
             dma("Y", T.yx[:, 0:2048], T.X[:, 0:2048], ["X"], ["o1"], "out")
             dma("Y", T.yx[:, 2048:4096], T.X[:, 2048:4096], ["X"], ["o1"], "out")
             dma("S", T.ye[:], T.YE[:, 0:TS], ["YE%d" % k for k in range(TS)], ["o2"], "out2")
-        landed(t, "c", "CI%d" % (t + 1))
-        landed(t, "z", "z0_%d" % (t + 1))
-        update(t + 1, *nxt)
 
-    act(T.YZ[:], T.ZF[:], AF.Identity, ["z0_%d" % TS], ["YZ"], bias=-129.0)
+    def spare(t):
+        if t == 1:
+            ts(T.IH[:], T.IH[:], col(0), None, A.is_equal, None, ["IH", "c0"], ["IH"])
+        if t == 2:
+            ts(T.IL[:], T.IL[:], col(0), None, A.subtract, None, ["IL", "c0"], ["IL"])
+        if t == 3:
+            tt(T.ID2[:, 0:256], T.IH[:], T.IL[:], A.mult, ["IH", "IL"], ["ID2a"])
+        if t == TS - 1:
+            ts(T.R16[:], T.PL[:, 128 * TS:128 * TS + 128], MAGIC, MAGIC, A.add, A.subtract, ["PL%d" % TS], ["R16"])
+            ts(T.R1[:, 8:136], T.R16[:], 1.0 / 8192, None, A.mult, None, ["R16"], ["R1"])
+        offers(t + 1, 0)
+        offers(t + 1, 1)
+
+    def partners(h):
+        update(TS, h)
+        o, n, sk, p = 64 * h, 128 * TS + 64 * h, "SL%d_%d" % (h, TS), 56 * h
+        ts(T.R16[:, o:o + 56], T.SL[:, n:n + 56], 16.0, None, A.mult, None, [sk], ["R16%d" % h, "R16"])
+        ts(T.OP[:, 128 + 4 * h:132 + 4 * h], T.SL[:, n + 56:n + 60], 256.0, None, A.add, None, [sk], ["OPf%d" % h])
+        tt(T.CC[:, o + 28:o + 56], T.R16[:, o + 28:o + 56], T.SL[:, n:n + 28], A.add, ["R16%d" % h, sk], ["CC%d" % h])
+        tt(T.CC[:, o:o + 28], T.R16[:, o:o + 28], T.SL[:, n + 28:n + 56], A.add, ["R16%d" % h, sk], ["CC%d" % h])
+        cp(T.OP[:, p:p + 56], T.CC[:, o:o + 56], ["CC%d" % h], ["OP%d" % h])
+        idk = ["ID2a", "ID2b", "OP%d" % h]
+        act(T.G2[:, 448 * h:448 * h + 448], T.ID2[:].indirect(T.OP[:, p + 28:p + 56]), AF.Copy, idk, ["G%d" % h])
+        cp(T.CL[:, 448 * h:448 * h + 448], T.ID2[:].indirect(T.OP[:, p:p + 28]), idk, ["Hh%d" % h, "CL0s", "CL0v"])
+        bank = "B%d" % (2 * h)
+        for s in range(7):
+            mm(T[bank][:, 0:64], T.ID[:], T.CL[:, 448 * h + 64 * s:448 * h + 64 * s + 64], s == 0, False, ["ID", "Hh%d" % h], [bank])
+        for s in range(7):
+            mm(T[bank][:, 0:64], T.ID[:], T.G2[:, 448 * h + 64 * s:448 * h + 64 * s + 64], False, s == 6, ["ID", "G%d" % h], [bank])
+
+    weave(chain(columns, 0, 0), chain(lists), per=1)
+    for t in range(TS):
+        weave(chain(gathers, t, 0), chain(columns, t, 1), lead=1, per=5)
+        gb = chain(gathers, t, 1)
+        weave(gb[:2], [])
+        weave(chain(escape, t, 0), [])
+        weave(chain(choose, t, 0), [])
+        weave(gb[2:3], chain(newz, t, 0))
+        weave(gb[3:], [])
+        weave(chain(spare, t), [])
+        weave(chain(escape, t, 1), [])
+        weave(chain(choose, t, 1), [])
+        nxt = chain(columns, t + 1, 0) if t < TS - 1 else chain(partners, 0)
+        weave(nxt[:2], chain(newz, t, 1), lead=1)
+        weave(chain(write, t), nxt[2:])
+
+    partners(1)
+    act(T.YZ[:], T.ZF[:], AF.Identity, ["za0_%d" % TS, "za1_%d" % TS], ["YZ"], bias=-129.0)
     dma("S", T.yz[:], T.YZ[:], ["YZ"], ["o2"], "out2")
-    n, ka, kb = 128 * TS, "SL%da" % TS, "SL%db" % TS
-    ts(T.R16[:, 0:112], T.SL[:, n:n + 112], 16.0, None, A.mult, None, [ka], ["R16"])
-    tt(T.CC[:, 56:112], T.R16[:, 56:112], T.SL[:, n:n + 56], A.add, ["R16", ka], ["CCb"])
-    tt(T.CC[:, 0:56], T.R16[:, 0:56], T.SL[:, n + 56:n + 112], A.add, ["R16", ka], ["CCa"])
-    idk = ["ID2a", "ID2b"]
-    cp(T.OP[:, 56:112], T.CC[:, 56:112], ["CCb"], ["OPb"])
-    cp(T.OP[:, 0:56], T.CC[:, 0:56], ["CCa"], ["OPa"])
-    taken(112)
-    tt(T.SL[:, n + 112:n + 120], T.DW[:, 237:349:14], T.R1[:, 112:120], A.add, ["DWs", "R1"], [kb])
-    ts(T.OP[:, 128:136], T.SL[:, n + 112:n + 120], 256.0, None, A.add, None, [kb], ["OPf"])
-    parts = [(0, 2), (2, 4), (4, 6), (6, 7)]
-    for n, (a, b) in enumerate(parts):
-        act(T.G2[:, 128 * a:128 * b], T.ID2[:].indirect(T.OP[:, 56 + 8 * a:56 + 8 * b]), AF.Copy, idk + ["OPb"], ["G%d" % n])
-        tt(T.CL[:, 128 * a:128 * b], T.ID2[:].indirect(T.OP[:, 8 * a:8 * b]), T.G2[:, 128 * a:128 * b], A.add,
-           idk + ["OPa", "G%d" % n], ["H%d" % n, "CL0s", "CL0v"])
-        for s in range(a, b):
-            mm(T.B7[:, 0:128], T.ID[:], T.CL[:, 128 * s:128 * s + 128], s == 0, s == 6, ["ID", "H%d" % n], ["B7"])
-    act(T.YF[:], T.ID2[:].indirect(T.OP[:, 128:136]), AF.Copy, idk + ["OPf"], ["YF"])
+    act(T.YF[:], T.ID2[:].indirect(T.OP[:, 128:136]), AF.Copy, ["ID2a", "ID2b", "OPf0", "OPf1"], ["YF"])
     dma("S", T.yf[:], T.YF[0:128:16, :], ["YF"], ["o2"], "out2")
-    ts(T.YP[:], T.B7[:, 0:128], col(0), None, A.add, None, ["B7", "c0"], ["YP"])
-    dma("S", T.yp[:], T.YP[:], ["YP"], ["o2"], "out2")
+    for h in range(2):
+        ts(T.YP[:, 64 * h:64 * h + 64], T["B%d" % (2 * h)][:, 0:64], col(0), None, A.add, None, ["B%d" % (2 * h), "c0"], ["YP"])
+    dma("Y", T.yp[:], T.YP[:], ["YP"], ["o1"], "out")
 
     dsem, dcount = {}, {}
     lastw, readers = {}, {}
     for n, o in enumerate(ops):
-        deps = set()
+        deps, after = set(), set()
         for k in o["r"]:
             for m in lastw.get(k, []):
                 deps.add(m)
@@ -387,7 +481,10 @@ def rank_program(g, core, T, topo):
                 twin = o["dma"] is not None and ops[m]["dma"] == o["dma"]
                 if not same and not twin and ops[m]["dma"] != "remote":
                     deps.add(m)
+                elif same:
+                    after.add(m)
         o["deps"] = deps if o["kind"] == "op" else set()
+        o["after"] = after - deps - {n}
         for k in o["r"]:
             readers.setdefault(k, []).append(n)
         for k in o["w"]:
@@ -399,6 +496,72 @@ def rank_program(g, core, T, topo):
         if o["dma"] not in (None, "remote"):
             dsem.setdefault(o["dma"], "d%d" % len(dsem))
             dcount[o["dma"]] = dcount.get(o["dma"], 0) + 16
+    def length(o):
+        k = (o["w"] or [""])[0]
+        if o["kind"] == "ext":
+            return 0.0, 0.0
+        if o["dma"] == "remote":
+            return 0.3, FAR
+        if o["dma"] is not None:
+            return 0.1, 3.0
+        if "cols" in o:
+            c = o["cols"] * {"d": 0.0013, "a": 0.00104, "B": 0.0006}[k[0]] + (0.06 if k[0] == "d" else 0.0)
+        elif o["q"] == "P":
+            c = 0.1 if k == "B7" else 0.045
+        elif o["q"] == "G":
+            c = 1.8 if k[:2] == "W2" else 0.35
+        else:
+            c = 0.07
+            r0 = (o["r"] or [""])[0]
+            for pre, v in LENGTHS:
+                if k.startswith(pre):
+                    c = v
+                    break
+            if k[:2] == "ay":
+                c = {"0": 0.47, "448": 0.34, "768": 0.14}[r0[4:]]
+        return c, c
+
+    sent = {o["sem"]: n for n, o in enumerate(ops) if o["dma"] == "remote"}
+    succ = [[] for _ in ops]
+    need = [0] * len(ops)
+    lens = [length(o) for o in ops]
+    for n, o in enumerate(ops):
+        edges = [(m, lens[m][1] + WAKE) for m in o["deps"]] + [(m, lens[m][0]) for m in o["after"]]
+        if o["kind"] == "ext":
+            edges = [(sent[o["sem"]], FAR)]
+        for m, lat in edges:
+            succ[m].append((n, lat))
+            need[n] += 1
+    order, cnt0 = [n for n in range(len(ops)) if need[n] == 0], list(need)
+    for n in order:
+        for m, _ in succ[n]:
+            cnt0[m] -= 1
+            if cnt0[m] == 0:
+                order.append(m)
+    way = [0.0] * len(ops)
+    for n in reversed(order):
+        way[n] = max([lens[n][1]] + [lat + way[m] for m, lat in succ[n]])
+        if ops[n]["dma"] == "remote" and (ops[n]["sem"][1:3] == "c0" or ops[n]["sem"] == "as0"):
+            way[n] += LEAD
+    ready, at, free, order = [n for n in range(len(ops)) if need[n] == 0], [0.0] * len(ops), {}, []
+    while ready:
+        start = {n: max(at[n], free.get(ops[n]["q"], 0.0)) for n in ready}
+        first = min(ready, key=lambda n: (start[n], -way[n], n))
+        q = ops[first]["q"]
+        pick = max((n for n in ready if ops[n]["q"] == q and start[n] <= start[first] + SLACK), key=lambda n: (way[n], -n))
+        ready.remove(pick)
+        order.append(pick)
+        if q is not None:
+            free[q] = start[pick] + lens[pick][0]
+        for m, lat in succ[pick]:
+            at[m] = max(at[m], start[pick] + lat)
+            need[m] -= 1
+            if need[m] == 0:
+                ready.append(m)
+    place = {m: n for n, m in enumerate(order)}
+    ops = [ops[m] for m in order]
+    for o in ops:
+        o["deps"] = {place[m] for m in o["deps"]}
     known = {q: {} for q in Q}
     for n, o in enumerate(ops):
         if o["kind"] != "op":

from concourse.mybir import AluOpType, AxisListType, ActivationFunctionType

TS, N, HOP = 5, 8, 3
F32, BF, I32, U16 = "float32", "bfloat16", "int32", "uint16"
WW = 1920


def _sb(n, d):
    return ("sbuf", [128, n], d)


SCRATCH = {
    "X": _sb(4096, BF), "W2": _sb(2 * WW, BF), "DX": _sb(1792, BF), "AY": _sb(1792, BF), "W1": _sb(2 * TS * WW, BF), "ZN": _sb(128 * TS, BF),
    "NMI": _sb(128, I32), "PRI": _sb(128, I32), "Z0": _sb(128, BF), "THI": _sb(8, I32), "TH": _sb(8, F32),
    "PI": _sb(8, I32), "PJ": _sb(8, I32), "COL": _sb(16, F32), "J": _sb(144, F32), "GI": _sb(128, F32),
    "Q": _sb(144, BF), "Q2": _sb(144, BF), "ID": _sb(128, BF), "IA": _sb(128, BF), "IB": _sb(128, BF), "IF": _sb(128, F32),
    "BO": _sb(128, BF), "LT1": _sb(128, BF), "LT2": _sb(128, BF), "LTF": _sb(128, F32), "NI": _sb(128, BF), "IF2": _sb(128, F32),
    "HI": _sb(128, I32), "LO": _sb(128, I32), "HIB": _sb(128, BF), "LOB": _sb(128, BF), "NZ": _sb(2048, BF), "CL": _sb(2048, BF),
    "LF": _sb(256, BF), "MM": _sb(256, BF), "W16": _sb(128, BF), "WK": _sb(128, BF), "WP": _sb(128, BF),
    "PN1": _sb(128, F32), "PN2": _sb(64, F32), "PN3": _sb(128, F32), "RN": _sb(128, F32), "ON": _sb(128, U16),
    "PTX": _sb(56, BF), "PTY": _sb(56, BF), "PAT": _sb(112, F32), "RST": _sb(112, F32), "CB": _sb(8, F32),
    "JJ": _sb(8, F32), "QI": _sb(8, I32), "QW": _sb(8, I32), "QF": _sb(8, F32), "QG": _sb(8, F32), "C2": _sb(8, F32), "C512": _sb(8, F32),
    "LFE": _sb(8, U16), "LC": _sb(8, U16), "LTP": _sb(8, U16), "L12": _sb(8, U16),
    "RP": _sb(128, BF), "WA": _sb(128, F32), "BL": _sb(128, F32), "HP": _sb(256, I32), "OFF": _sb(224, U16),
    "K2": _sb(128, F32), "K1": _sb(128, F32), "MI": _sb(8, I32), "M2": _sb(8, I32), "OZ": _sb(8, U16),
    "TT": _sb(256, F32), "MK": _sb(224, F32), "DW": _sb(464, F32), "TZ": _sb(128, F32),
    "UI": _sb(8, I32), "CU": _sb(8, U16), "TA": _sb(128, BF), "M129": _sb(128, BF), "EB": _sb(8, BF), "EJ": _sb(8, F32),
    "YE": _sb(8, F32), "AI": _sb(4, I32), "A63": _sb(4, F32),
    "IH": _sb(256, BF), "IL": _sb(256, BF), "ID2": _sb(272, BF), "R16": _sb(128, F32), "R1": _sb(136, F32), "CC": _sb(128, F32),
    "OP": _sb(136, U16), "YP": _sb(128, F32), "YF": _sb(128, F32), "YZ": _sb(128, BF), "ZF": _sb(128, BF),
    "DG": _sb(128, BF), "R16S": _sb(128, F32), "US": _sb(128, F32), "G2": _sb(896, BF),
    "SL": _sb(128 * (TS + 1), F32), "PL": _sb(128 * (TS + 1), F32), "CI": _sb(16 * (TS + 1), I32), "CO": _sb(16 * TS, I32),
}
for _t in range(8):
    SCRATCH["B%d" % _t] = ("psum", [128, 512], F32)

SEMAPHORES = (["cV", "cS", "cP", "cG", "left"] + ["d%d" % i for i in range(24)]
              + ["a%s%d" % (k, i) for k in ("z0", "z1", "c0", "c1", "s") for i in range(TS)])

A = AluOpType
AF = ActivationFunctionType
MAGIC = float(3 * 2 ** 35)
FAR, WAKE, SLACK, LEAD = 3.6, 0.15, 0.03, 2.0
XC = [("B7", 512, 896), ("V", 0, 512)]
LENGTHS = [("dxs", 0.56), ("dx", 0.72), ("dy0_0", 0.63), ("dy1_0", 0.63), ("dy0_4", 0.46), ("dy1_4", 0.46), ("dy", 0.22), ("ax", 0.47),
           ("MK", 0.2), ("DWd", 0.2), ("DWs", 0.12), ("SL", 0.13), ("TT", 0.13), ("WA", 0.13), ("Hh", 0.63), ("H", 0.12), ("of", 0.12),
           ("TA", 0.15), ("X", 0.47), ("US", 0.13), ("ZN", 0.13), ("TZ", 0.15), ("zb", 0.16), ("NZ", 1.06), ("CL0s", 0.73), ("CL0v", 0.72),
           ("CL1s", 0.73), ("CL1v", 0.72), ("G", 0.65), ("MM", 0.27), ("W16", 0.27), ("WP", 0.27), ("LT", 0.2), ("LF", 0.13), ("ID2a", 0.53),
           ("I", 0.13), ("Q2", 0.15), ("BO", 0.13), ("LO", 0.13), ("YF", 0.23), ("YZ", 0.13), ("R1", 0.13), ("DG", 0.13), ("NI", 0.13)]


def rank_program(g, core, T, topo):
    rank = T.rank_of(core)
    if rank is None:
        return
    Q = {"V": g.vector, "S": g.scalar, "P": g.tensor, "G": g, "Y": g.sync}
    ops = []
    sink = [ops]

    def op(q, fn, r=(), w=(), dma=None):
        sink[0].append({"q": q, "fn": fn, "r": list(r), "w": list(w), "dma": dma, "kind": "op"})

    def ops_n(k, n):
        for o in sink[0][-k:]:
            o["cols"] = n

    def chain(fn, *args):
        sink[0] = []
        fn(*args)
        calls, out = sink[0], [[]]
        sink[0] = ops
        for c in calls:
            if c["q"] == "V" and any(d["q"] == "V" for d in out[-1]):
                out.append([])
            out[-1].append(c)
        return out

    def weave(a, b, lead=0, per=1):
        a, b = list(a), list(b)
        n = 0
        while a or b:
            if a:
                ops.extend(a.pop(0))
            n += 1
            if n > lead or not a:
                for _ in range(per):
                    if b:
                        ops.extend(b.pop(0))

    def ts(out, in0, s1, s2, o0, o1, r, w):
        if o1 is None:
            op("V", lambda: g.vector.tensor_scalar(out, in0, s1, None, o0), r, w)
        else:
            op("V", lambda: g.vector.tensor_scalar(out, in0, s1, s2, o0, o1), r, w)

    def tt(out, in0, in1, o, r, w):
        op("V", lambda: g.vector.tensor_tensor(out, in0, in1, o), r, w)

    def cp(out, in_, r, w):
        op("V", lambda: g.vector.tensor_copy(out, in_), r, w)

    def ms(out, c, w):
        op("V", lambda: g.vector.memset(out, c), [], w)

    def rmax(out, in_, r, w):
        op("V", lambda: g.vector.tensor_reduce(out, in_, AxisListType.X, A.max), r, w)

    def scan(out, d0, d1, o1, r, w):
        op("V", lambda: g.vector.tensor_tensor_scan(out, d0, d1, 0.0, A.mult, o1), r, w)

    def act(out, in_, f, r, w, bias=0.0, scale=1.0, acc=None):
        if acc is None:
            op("S", lambda: g.scalar.activation(out, in_, f, bias=bias, scale=scale), r, w)
        else:
            op("S", lambda: g.scalar.activation(out, in_, f, bias=bias, scale=scale, accum_out=acc), r, w)

    def mm(out, l, rh, st, sp, r, w):
        op("P", lambda: g.tensor.matmul(out, l, rh, st, sp), r, w)

    def iota(out, pat, base, cm, w, isint=False):
        if isint:
            op("G", lambda: g.iota(out, pat, base, cm), [], w)
        else:
            op("G", lambda: g.iota(out, pat, base, cm, allow_small_or_imprecise_dtypes=True), [], w)

    def dma(q, out, in_, r, w, grp):
        op(q, lambda: Q[q].dma_start(out, in_), r, w, dma=grp)

    def fold(bank, n, sel, data, c0, r):
        for b in range(16):
            mm(T[bank][:, 0:n], sel[:, 15 - b:143 - b], data[:, c0 + b:c0 + 16 * n:16], False, b == 15, r, [bank])

    left = [0]

    def send(t, kind, dst, src, r):
        to = T.cores[(rank + (HOP if t < TS - 1 else -HOP * (TS - 1))) % N]
        rid, pid, _ = topo.addr(to)
        mask = topo.mask(core, to)
        left[0] += len(topo.engines(core, to))
        op("G", lambda: g.remote_dma(dst, src, T.sem["a%s%d" % (kind, t)], T.sem.left, pid, rid, mask), r, [], dma="remote")
        sink[0][-1]["sem"] = "a%s%d" % (kind, t)

    for t in range(TS):
        frm = T.cores[(rank - (HOP if t < TS - 1 else -HOP * (TS - 1))) % N]
        for kind, key in (("s", "PL%d"), ("c0", "CI0_%d"), ("c1", "CI1_%d"), ("z0", "za0_%d"), ("z1", "za1_%d")):
            ops.append({"q": None, "r": [], "w": [key % (t + 1)], "kind": "ext", "sem": "a%s%d" % (kind, t),
                        "n": len(topo.engines(frm, core)), "dma": None})

    col = lambda j: T.COL[:, j:j + 1]

    dma("Y", T.PRI[:], T.pr[:], [], ["PRI"], "pr")
    dma("S", T.NMI[:], T.nm[:], [], ["NMI"], "nm")
    dma("Y", T.X[:, 0:2048], T.xt[:, 0:2048], [], ["X"], "x")

    iota(T.PI[:, 0:1], [[0, 1]], 0, 1, ["PI"], True)
    iota(T.J[:], [[1, 144]], 0, -1, ["J"])
    iota(T.GI[:], [[1, 8], [0, 16]], 0, 0, ["GI"])
    for h in range(2):
        iota(T.PN1[:, 64 * h:64 * h + 56], [[0, 2], [1920, 7], [-1, 4]], 3072 - 4 * h, 0, ["PN1"])
        iota(T.PN1[:, 64 * h + 56:64 * h + 64], [[1920, 2], [-1, 4]], 1920 * 8 + 1152 - 4 * h, 0, ["PN1"])
    iota(T.PN2[:], [[0, 64]], -2, 0, ["PN2"])
    iota(T.PN3[:], [[4096, 2], [0, 16], [1024, 4]], 0, 0, ["PN3"])
    iota(T.JJ[:], [[16, 8]], 0, 0, ["JJ"])
    iota(T.C2[:], [[4, 8]], 0, 0, ["C2"])
    iota(T.C512[:], [[512, 8]], 0, 0, ["C512"])
    iota(T.PTX[:], [[1, 56]], 64, 0, ["PTX"])
    iota(T.PTY[:], [[0, 2], [8, 7], [2, 4]], 92, 0, ["PTY"])
    iota(T.BL[:], [[0, 128]], 0, 0, ["BL0", "BL1"])
    iota(T.PAT[:, 0:56], [[1, 4], [4, 14]], 0, 0, ["PAT"])
    iota(T.PAT[:, 56:112], [[1, 4], [-28, 2], [4, 7]], 92, 0, ["PAT"])
    iota(T.RST[:], [[0, 8], [1, 14]], 0, 0, ["RST0"])
    iota(T.R16S[:], [[0, 8], [1, 16]], 0, 0, ["R16S0"])
    iota(T.M129[:], [[0, 128]], -129, 0, ["M129"])
    iota(T.PL[:, 120:128], [[0, 8]], 0, 0, ["pad"])
    iota(T.R1[:, 0:8], [[0, 8]], 0, 0, ["pad"])
    for h in range(2):
        iota(T.DW[:, 232 * h + 112:232 * h + 120], [[0, 8]], 0, 0, ["DWz"])
        iota(T.W2[:, WW * h + 896:WW * h + WW], [[0, 1024]], 129, 0, ["W2c%d" % h])
    iota(T.IH[:], [[1, 16], [0, 16]], 0, 0, ["IH"])
    iota(T.IL[:], [[0, 16], [1, 16]], 0, 0, ["IL"])
    iota(T.ID2[:, 256:272], [[1, 16]], 0, 0, ["ID2b"])

    ms(T.NZ[:], 0.0, ["NZ"])
    ts(T.PJ[:, 0:1], T.PI[:, 0:1], 15, None, A.bitwise_and, None, ["PI"], ["PJ0"])
    ts(T.PJ[:, 1:2], T.PI[:, 0:1], 4, None, A.arith_shift_right, None, ["PI"], ["PJ1"])
    ts(T.PJ[:, 2:3], T.PI[:, 0:1], 3, None, A.bitwise_and, None, ["PI"], ["PJ2"])
    ts(T.PJ[:, 3:4], T.PI[:, 0:1], 2, 3, A.arith_shift_right, A.bitwise_and, ["PI"], ["PJ3"])
    cp(T.COL[:, 0:4], T.PJ[:, 0:4], ["PJ0", "PJ1", "PJ2", "PJ3"], ["c0"])
    ts(T.LTF[:], T.J[:, 0:128], 0.0, 16.0, A.is_ge, A.mult, ["J"], ["LTF"])
    ts(T.ID[:], T.J[:, 0:128], 0.0, None, A.is_equal, None, ["J"], ["ID"])
    ts(T.BO[:], T.GI[:], col(1), None, A.is_equal, None, ["GI", "c0"], ["BO"])
    ts(T.IF[:], T.J[:, 0:128], 0.0, 112.0, A.is_equal, A.mult, ["J"], ["IF"])
    ts(col(4), col(0), -1.0, 15.0, A.mult, A.add, ["c0"], ["c4"])
    tt(T.LT1[:], T.LTF[:], T.BO[:], A.mult, ["LTF", "BO"], ["LT1"])
    ts(T.IF2[:], T.J[:, 0:128], 0.0, 1024.0, A.is_equal, A.mult, ["J"], ["IF2"])
    tt(T.LT2[:], T.LT1[:], T.IF[:], A.add, ["LT1", "IF"], ["LT2"])

    ts(T.LF[:, 0:128], T.PRI[:], col(0), None, A.is_gt, None, ["PRI", "c0"], ["LFa"])
    ts(T.LF[:, 128:256], T.PRI[:], col(0), None, A.is_equal, None, ["PRI", "c0"], ["LFb"])
    mm(T.B7[:, 0:128], T.LT1[:], T.LF[:, 0:128], True, True, ["LT1", "LFa"], ["B7"])
    mm(T.B7[:, 128:256], T.LT2[:], T.LF[:, 128:256], True, True, ["LT2", "LFb"], ["B7"])
    ts(T.HI[:], T.NMI[:], 6, None, A.arith_shift_right, None, ["NMI"], ["HI"])
    ts(T.LO[:], T.NMI[:], 63, None, A.bitwise_and, None, ["NMI"], ["LO"])
    cp(T.HIB[:], T.HI[:], ["HI"], ["HIB"])
    cp(T.LOB[:], T.LO[:], ["LO"], ["LOB"])
    dma("S", T.NZ[0:128:16, :], T.HIB[:], ["HIB"], ["NZ"], "nz")
    dma("S", T.NZ[1:128:16, :], T.LOB[:], ["LOB"], ["NZ"], "nz")
    dma("S", T.Z0[:], T.z0[:], [], ["Z0"], "z0")
    dma("S", T.X[:, 2048:4096], T.xt[:, 2048:4096], [], ["X"], "x")
    dma("S", T.THI[:, 0:TS], T.th[:], [], ["THI"], "th")
    tt(T.MM[:], T.B7[:, 0:256], T.LF[:], A.mult, ["B7", "LFa", "LFb"], ["MM"])
    ts(T.Q[:], T.J[:], col(4), -8192.0, A.is_equal, A.mult, ["J", "c4"], ["Q"])
    tt(T.W16[:], T.MM[:, 0:128], T.MM[:, 128:256], A.add, ["MM"], ["W16"])
    ts(col(5), col(0), 0.0, 63.0, A.is_equal, A.mult, ["c0"], ["c5"])
    ts(T.WK[:], T.W16[:], col(0), None, A.add, None, ["W16", "c0"], ["WK"])
    tt(T.WP[:], T.W16[:], T.PRI[:], A.add, ["W16", "PRI"], ["WP"])
    for h in range(2):
        mm(T["B%d" % (2 * h)][:, 0:64], T.IF2[:], T.PN1[:, 64 * h:64 * h + 64], True, False, ["IF2", "PN1"], ["B%d" % (2 * h)])
        mm(T["B%d" % (2 * h + 1)][:, 0:64], T.IF2[:], T.PN2[:], True, False, ["IF2", "PN2"], ["B%d" % (2 * h + 1)])
    for h in range(2):
        for s in range(16):
            j = s + 1 if s < 7 else s - 6
            src = "WP" if 7 <= s < 14 else "WK"
            o = 1024 * h + 64 * s
            ts(T.CL[:, o:o + 64], T[src][:, 64 * h:64 * h + 64], 16.0 * j, 16.0 * j + 16.0, A.max, A.min, [src], ["CL%d" % h])
        fold("B%d" % (2 * h), 64, T.Q, T.CL, 1024 * h, ["Q", "CL%d" % h])
    ts(col(9), col(0), 2.0, None, A.is_lt, None, ["c0"], ["c9"])
    ts(T.LFE[:, 0:4], T.J[:, 0:4], 0.0, col(2), A.mult, A.add, ["J", "c0"], ["LFE"])
    tt(col(5), col(5), col(9), A.add, ["c5", "c9"], ["c5"])
    ts(T.LFE[:, 4:8], T.GI[:, 64:68], col(2), None, A.add, None, ["GI", "c0"], ["LFE"])
    ts(T.Q2[:], T.J[:], col(4), col(5), A.is_equal, A.mult, ["J", "c4", "c5"], ["Q2"])
    for h in range(2):
        bank, on, o = "B%d" % (2 * h), "ON%d" % h, 64 * h
        ts(T.ON[:, o:o + 64], T[bank][:, 0:64], -1.0 / 64, col(0), A.mult, A.add, [bank, "c0"], [on])
        act(T.CL[:, 16 * o:16 * o + 512], T.NZ[:].indirect(T.ON[:, o:o + 32]), AF.Copy, ["NZ", on], ["CL%ds" % h])
        cp(T.CL[:, 16 * o + 512:16 * o + 1024], T.NZ[:].indirect(T.ON[:, o + 32:o + 64]), ["NZ", on], ["CL%dv" % h])
        act(T.RN[:, o:o + 64], T[bank][:, 0:64], AF.Identity, [bank], ["RN%d" % h], scale=-1.0)
        fold("B%d" % (2 * h + 1), 64, T.Q2, T.CL, 1024 * h, ["Q2", "CL%ds" % h, "CL%dv" % h])
    for h in range(2):
        act(T.W1[:, WW * h:WW * h + 64], T.Z0[:, 64 * h:64 * h + 64], AF.Identity, ["Z0"], ["za%d_0" % h], bias=129.0)
    ts(T.IA[:], T.J[:, 0:128], 0.0, -1.0 / 32, A.is_equal, A.mult, ["J"], ["IA"])
    ts(T.IB[:], T.J[:, 0:128], 0.0, -1.0 / 16, A.is_equal, A.mult, ["J"], ["IB"])
    ms(T.A63[:], 0.0, ["A63"])
    ts(T.NI[:], T.J[:, 0:128], 0.0, -1.0, A.is_equal, A.mult, ["J"], ["NI"])
    tt(T.RP[:], T.RN[:], T.PN3[:], A.subtract, ["RN0", "RN1", "PN3"], ["RP0", "RP1"])

    def lists():
        ts(T.JJ[:], T.JJ[:], col(0), None, A.add, None, ["JJ", "c0"], ["JJ"])
        ts(col(6), col(2), 14.0, col(3), A.mult, A.add, ["c0"], ["c6"])
        ts(T.QI[:], T.JJ[:], -6.5, 1.0 / 14, A.add, A.mult, ["JJ"], ["QI"])
        ts(col(8), col(0), 32.0, None, A.mult, None, ["c0"], ["c8"])
        ts(T.QW[:], T.QI[:], 2, None, A.arith_shift_right, None, ["QI"], ["QW"])
        ts(T.QF[:], T.QI[:], -55.0, None, A.mult, None, ["QI"], ["QF"])
        ts(T.JJ[:], T.JJ[:], 4.0, None, A.mult, None, ["JJ", "QI"], ["JJ"])
        cp(T.LC[:], T.QI[:], ["QI"], ["LC"])
        ts(T.QG[:], T.QW[:], 60.0, None, A.mult, None, ["QW"], ["QG"])
        tt(T.QF[:], T.QF[:], T.JJ[:], A.add, ["QF", "JJ"], ["QF"])
        ts(T.L12[:, 0:3], T.C2[:, 0:3], col(6), None, A.add, None, ["C2", "c6"], ["L12"])
        tt(T.QF[:], T.QF[:], T.QG[:], A.add, ["QF", "QG"], ["QF"])
        ts(T.L12[:, 4:7], T.C2[:, 0:3], col(6), 56.0, A.add, A.add, ["C2", "c6"], ["L12"])
        ts(T.CB[:], T.C512[:], col(8), None, A.add, None, ["C512", "c8"], ["CB"])
        cp(T.LTP[:], T.QF[:], ["QF"], ["LTP"])
        ts(col(10), col(3), 2.0, 119.0, A.is_ge, A.mult, ["c0"], ["c10"])
        ts(col(11), col(3), 3.0, 55.0, A.is_ge, A.mult, ["c0"], ["c11"])
        ts(col(12), col(6), -1.0, 44.0, A.mult, A.add, ["c6"], ["c12"])
        ts(col(10), col(10), col(11), 12.0, A.add, A.add, ["c10", "c11"], ["c10"])
        ts(col(12), col(3), 2.0, col(12), A.is_ge, A.mult, ["c0", "c12"], ["c12"])
        ts(T.L12[:, 3:4], col(10), col(6), None, A.add, None, ["c10", "c6"], ["L12"])
        ts(T.L12[:, 7:8], col(12), col(6), 68.0, A.add, A.add, ["c12", "c6"], ["L12"])
        ts(T.TH[:, 0:TS], T.THI[:, 0:TS], 8192.0, 256.0, A.mult, A.add, ["THI"], ["TH"])
        ts(T.DG[:], T.R16S[:], col(0), 4096.0, A.is_equal, A.mult, ["R16S0", "c0"], ["DG"])
        ts(T.RST[:], T.RST[:], 1.0, None, A.min, None, ["RST0"], ["RST"])
        ts(T.R16S[:], T.R16S[:], 1.0, None, A.min, None, ["R16S0", "DG"], ["R16S"])

    def before(t, h):
        return (T.PL, 128 * t + 64 * h, "PL%d" % t) if t < TS else (T.R1, 64 * h + 8, "R1")

    def offers(t, h):
        buf, o, key = before(t, h)
        for w in range(2):
            c = 128 * h + 64 * w
            tt(T.TT[:, c:c + 64], buf[:, o + 56:o + 64].indirect(T.LFE[:, 4 * w:4 * w + 4]), buf[:, o - 8:o + 56], A.subtract, [key, "LFE", "pad"], ["TT%d" % h])

    def update(t, h):
        buf, o, key = before(t, h)
        n, sk, d, ci = 128 * t + 64 * h, "SL%d_%d" % (h, t), 232 * h, 16 * t + 8 * h
        mk, dw = T.MK[:, 112 * h:112 * h + 112], T.DW[:, d:d + 112]
        tt(mk, T.CI[:, ci:ci + 8].indirect(T.LC[:, 0:7]), T.PAT[:], A.is_equal, ["CI%d_%d" % (h, t), "LC", "PAT"], ["MK%d" % h])
        tt(dw, T.TT[:, 128 * h + 8:128 * h + 128].indirect(T.LTP[:, 0:7]), mk, A.mult, ["TT%d" % h, "LTP", "MK%d" % h], ["DWd%d" % h])
        scan(T.DW[:, d + 120:d + 232], T.RST[:], dw, A.subtract, ["RST", "DWd%d" % h], ["DWs%d" % h])
        tt(T.SL[:, n:n + 64], T.DW[:, d:d + 120].indirect(T.L12[:, 4:8]), buf[:, o:o + 64], A.add, ["DWd%d" % h, "DWz", "L12", key], [sk])
        tt(T.SL[:, n:n + 64], T.DW[:, d:d + 232].indirect(T.L12[:, 0:4]), T.SL[:, n:n + 64], A.add, ["DWd%d" % h, "DWs%d" % h, "DWz", "L12", sk], [sk])

    def columns(t, h):
        o, n, sk, w = 64 * h, 128 * t + 64 * h, "SL%d_%d" % (h, t), WW * (2 * t + h)
        wa, rp, bl, za, z4, z16 = "WA%d" % h, "RP%d" % h, "BL%d" % h, "za%d_%d" % (h, t), "zb%d_%d" % (h, t), "zc%d_%d" % (h, t)
        if t > 0:
            update(t, h)
            if h == 1:
                send(t, "s", T.PL[:, 128 * t + 128:128 * t + 256], T.SL[:, 128 * t:128 * t + 128], ["SL0_%d" % t, sk])
            ts(T.RP[:, o:o + 64], T.SL[:, n:n + 64], MAGIC, MAGIC, A.add, A.subtract, [sk], [rp])
        for k in (64, 128, 256):
            act(T.W1[:, w + k:w + 2 * k], T.W1[:, w:w + k], AF.Copy, [za, z4], [z4])
        dma("Y", T.W1[:, w + 512:w + 1024], T.W1[:, w:w + 512], [za, z4], [z16], z16)
        if t > 0:
            tt(T.WA[:, o:o + 64], T.SL[:, n:n + 64], T.RP[:, o:o + 64], A.subtract, [sk, rp], [wa])
        else:
            cp(T.WA[:, o:o + 64], T["B%d" % (2 * h + 1)][:, 0:64], ["B%d" % (2 * h + 1)], [wa])
        px, py = "B%d" % (2 * h), "B%d" % (2 * h + 1)
        mm(T[px][:, 0:56], T.ID[:], T.PTX[:], True, False, ["ID", "PTX"], [px])
        mm(T[px][:, 0:56], T.IA[:], T.RP[:, o:o + 56], False, False, ["IA", rp], [px])
        mm(T[py][:, 0:56], T.ID[:], T.PTY[:], True, False, ["ID", "PTY"], [py])
        mm(T[py][:, 0:28], T.IB[:], T.RP[:, o + 28:o + 56], False, False, ["IB", rp], [py])
        mm(T[py][:, 28:56], T.IB[:], T.RP[:, o:o + 28], False, False, ["IB", rp], [py])
        ts(T.BL[:, o:o + 28], T.WA[:, o + 28:o + 56], 3232.0, None, A.add, None, [wa], [bl])
        for k in (0, 56):
            act(T.B4[:, k:k + 28], T.WA[:, o + 28:o + 56], AF.Identity, [wa, "A63"], ["B4"], bias=T.A63[:, 0:1], scale=2400.0)
            act(T.B4[:, k + 28:k + 56], T.WA[:, o:o + 28], AF.Identity, [wa, "A63"], ["B4"], bias=T.A63[:, 0:1], scale=2400.0)
        ts(T.BL[:, o + 28:o + 56], T.WA[:, o:o + 28], 3232.0, None, A.add, None, [wa], [bl])
        hp, hk = 128 * h, "H%d" % h
        tt(T.HP[:, hp + 56:hp + 120], T.WA[:, o + 56:o + 64].indirect(T.LFE[:, 0:4]), T.BL[:, o:o + 64], A.mult, [wa, bl, "LFE"], [hk + "y"])
        tt(T.HP[:, hp:hp + 56], T.WA[:, o:o + 56], T.BL[:, o:o + 56], A.mult, [wa, bl], [hk])
        hh = T.HP[:, hp:hp + 112]
        tt(hh, hh, T.B4[:, 0:112], A.add, [hk, hk + "y", "B4"], [hk])
        ts(hh, hh, 5, 4095, A.arith_shift_right, A.bitwise_and, [hk], [hk])
        cp(T.OFF[:, 112 * h:112 * h + 112], hh, [hk], ["of%d" % h])
        if t == 0:
            tt(T.SL[:, o:o + 64], T.WA[:, o:o + 64], T.RP[:, o:o + 64], A.add, [wa, rp], [sk])
            if h == 1:
                send(t, "s", T.PL[:, 128:256], T.SL[:, 0:128], ["SL0_0", sk])

    def gathers(t, h):
        w, d, f, of = WW * (2 * t + h), 896 * h, 112 * h, "of%d" % h
        zr = ["za%d_%d" % (h, t), "zb%d_%d" % (h, t)]
        px, py = "B%d" % (2 * h), "B%d" % (2 * h + 1)
        axs = []
        for e, a, b in XC:
            k, ax = "dx%s%d_%d" % (e[0], h, a), "ax%d_%d_%d" % (h, t, a)
            axs.append(ax)
            src = T.X[:].indirect(T.OFF[:, f + a // 16:f + b // 16])
            if e == "V":
                tt(T.DX[:, d + a:d + b], src, T.W1[:, w:w + b - a], A.subtract, ["X", of] + zr, [k])
                act(T.W1[:, w + 1024 + a:w + 1024 + b], T.DX[:, d + a:d + b], AF.Abs, [k], [ax], bias=129.0)
                ops_n(2, b - a)
            else:
                act(T.DX[:, d + a:d + b], src, AF.Copy, ["X", of], [k])
                mm(T[e][:, 0:b - a], T.NI[:], T.W1[:, w:w + b - a], True, False, ["NI"] + zr, [e])
                mm(T[e][:, 0:b - a], T.ID[:], T.DX[:, d + a:d + b], False, True, ["ID", k], [e])
                act(T.W1[:, w + 1024 + a:w + 1024 + b], T[e][:, 0:b - a], AF.Abs, [e], [ax], bias=129.0)
                ops_n(4, b - a)
        fold(px, 56, T.Q, T.W1, w + 1024, ["Q"] + axs)
        for a, b in ((0, 448), (448, 768), (768, 896)):
            k = "dy%d_%d" % (h, a)
            tt(T.W2[:, WW * h + a:WW * h + b], T.X[:].indirect(T.OFF[:, f + 56 + a // 16:f + 56 + b // 16]), T.W1[:, w:w + b - a], A.subtract, ["X", of] + zr, [k])
            act(T.AY[:, d + a:d + b], T.W2[:, WW * h + a:WW * h + b], AF.Abs, [k], ["ay%d" % h], bias=129.0)
        fold(py, 56, T.Q, T.AY, d, ["Q", "ay%d" % h])
        act(T.K2[:, 64 * h:64 * h + 28], T[px][:, 28:56], AF.Copy, [px], ["K2%d" % h])
        act(T.K2[:, 64 * h + 28:64 * h + 56], T[px][:, 0:28], AF.Copy, [px], ["K2%d" % h])

    def escape(t, h):
        o = 64 * h
        m2 = T.M2[:, 4 * h:4 * h + 4]
        for a in range(4):
            rmax(T.M2[:, 4 * h + a:4 * h + a + 1], T.K2[:, o + a:o + 56:4], ["K2%d" % h], ["M2%d" % h])
        ts(m2, m2, 127, None, A.bitwise_and, None, ["M2%d" % h], ["M2%d" % h])
        ts(T.K1[:, o + 56:o + 60], m2, T.TH[:, t:t + 1], None, A.add, None, ["M2%d" % h, "TH"], ["K1c%d" % h])

    def choose(t, h):
        o, w, co, py = 64 * h, WW * (2 * t + h), 16 * t + 8 * h, "B%d" % (2 * h + 1)
        mi, oz, k7, k8 = T.MI[:, 4 * h:4 * h + 4], T.OZ[:, 4 * h:4 * h + 4], "C7%d_%d" % (h, t), "C8%d_%d" % (h, t)
        tt(T.K1[:, o:o + 56], T[py][:, 0:56], T.K2[:, o:o + 56], A.subtract, [py, "K2%d" % h], ["K1%d" % h])
        for a in range(4):
            rmax(T.MI[:, 4 * h + a:4 * h + a + 1], T.K1[:, o + a:o + 60:4], ["K1%d" % h, "K1c%d" % h], ["MI%d" % h])
        c7, c8 = T.CO[:, co:co + 4], T.CO[:, co + 4:co + 8]
        ts(c8, mi, 127, None, A.bitwise_and, None, ["MI%d" % h], [k8])
        ts(c7, mi, 63, None, A.bitwise_and, None, ["MI%d" % h], [k7])
        send(t, "c%d" % h, T.CI[:, co + 16:co + 24], T.CO[:, co:co + 8], [k7, k8])
        ts(oz, c8, 16.0, col(0), A.mult, A.add, [k8, "c0"], ["OZ%d" % h])
        dys = ["dy%d_%d" % (h, a) for a in (0, 448, 768)]
        act(T.TZ[:, o:o + 64], T.W2[:, WW * h:WW * h + WW].indirect(oz), AF.Identity, ["OZ%d" % h, "W2c%d" % h] + dys, ["TZ%d" % h], bias=64.25, scale=0.5)
        ts(T.EB[:, 4 * h:4 * h + 4], c8, 64.0, None, A.is_ge, None, [k8], ["EB%d" % h])
        if h == 1:
            mm(T.B5[:, 0:128], T.ID[:], T.DG[:], True, False, ["ID", "DG"], ["B5"])
            mm(T.B6[:, 0:8], T.BO[:], T.EB[:], True, True, ["BO", "EB0", "EB1"], ["B6"])
            act(T.EJ[:], T.B6[:, 0:8], AF.Identity, ["B6"], ["EJ", "YE%d" % t], acc=T.YE[:, t:t + 1])

    def newz(t, h):
        o, w = 64 * h, WW * (2 * t + h)
        zn, k = T.ZN[:, 128 * t + o:128 * t + o + 64], "ZN%d_%d" % (h, t)
        tt(zn, T.W1[:, w:w + WW].indirect(T.OZ[:, 4 * h:4 * h + 4]), T.TZ[:, o:o + 64], A.add,
           ["OZ%d" % h, "TZ%d" % h, "za%d_%d" % (h, t), "zb%d_%d" % (h, t), "zc%d_%d" % (h, t)] + ["ax%d_%d_%d" % (h, t, a) for _, a, _b in XC], [k])
        send(t, "z%d" % h, T.W1[:, w + 2 * WW:w + 2 * WW + 64] if t < TS - 1 else T.ZF[:, o:o + 64], zn, [k])

    def write(t):
        zn, zk = T.ZN[:, 128 * t:128 * t + 128], ["ZN0_%d" % t, "ZN1_%d" % t]
        mm(T.B5[:, 0:128], T.BO[:], zn, False, True, ["BO"] + zk, ["B5"])
        if t < TS - 1:
            ts(T.AI[:, 0:1], T.YE[:, t:t + 1], 32.0, T.A63[:, 0:1], A.mult, A.add, ["YE%d" % t, "A63"], ["AI"])
            ts(T.AI[:, 0:1], T.AI[:, 0:1], 63 * 32, None, A.bitwise_and, None, ["AI"], ["AI"])
            cp(T.A63[:, 0:1], T.AI[:, 0:1], ["AI"], ["A63"])
        scan(T.US[:], T.R16S[:], T.B5[:, 0:128], A.max, ["R16S", "B5"], ["US"])
        ts(T.UI[:], T.US[:, 15:128:16], -2064.0 - 4096.0, None, A.add, None, ["US"], ["UI"])
        ts(T.UI[:], T.UI[:], 31, None, A.bitwise_and, None, ["UI"], ["UI"])
        tt(T.UI[:], T.UI[:], T.CB[:], A.add, ["UI", "CB"], ["UI"])
        cp(T.CU[:], T.UI[:], ["UI"], ["CU"])
        tt(T.TA[:], T.X[:].indirect(T.CU[:]), zn, A.add, ["X", "CU"] + zk, ["TA"])
        ts(T.TA[:], T.TA[:], 0.5, 64.25, A.mult, A.add, ["TA"], ["TA"])
        tt(T.X[:].indirect(T.CU[:]), T.TA[:], T.M129[:], A.add, ["TA", "CU", "M129"], ["X"])
        if t == TS - 1:
            dma("Y", T.yx[:, 0:2048], T.X[:, 0:2048], ["X"], ["o1"], "out")
            dma("Y", T.yx[:, 2048:4096], T.X[:, 2048:4096], ["X"], ["o1"], "out")
            dma("S", T.ye[:], T.YE[:, 0:TS], ["YE%d" % k for k in range(TS)], ["o2"], "out2")

    def spare(t):
        if t == 1:
            ts(T.IH[:], T.IH[:], col(0), None, A.is_equal, None, ["IH", "c0"], ["IH"])
        if t == 2:
            ts(T.IL[:], T.IL[:], col(0), None, A.subtract, None, ["IL", "c0"], ["IL"])
        if t == 3:
            tt(T.ID2[:, 0:256], T.IH[:], T.IL[:], A.mult, ["IH", "IL"], ["ID2a"])
        if t == TS - 1:
            ts(T.R16[:], T.PL[:, 128 * TS:128 * TS + 128], MAGIC, MAGIC, A.add, A.subtract, ["PL%d" % TS], ["R16"])
            ts(T.R1[:, 8:136], T.R16[:], 1.0 / 8192, None, A.mult, None, ["R16"], ["R1"])
        offers(t + 1, 0)
        offers(t + 1, 1)

    def partners(h):
        update(TS, h)
        o, n, sk, p = 64 * h, 128 * TS + 64 * h, "SL%d_%d" % (h, TS), 56 * h
        ts(T.R16[:, o:o + 56], T.SL[:, n:n + 56], 16.0, None, A.mult, None, [sk], ["R16%d" % h, "R16"])
        ts(T.OP[:, 128 + 4 * h:132 + 4 * h], T.SL[:, n + 56:n + 60], 256.0, None, A.add, None, [sk], ["OPf%d" % h])
        tt(T.CC[:, o + 28:o + 56], T.R16[:, o + 28:o + 56], T.SL[:, n:n + 28], A.add, ["R16%d" % h, sk], ["CC%d" % h])
        tt(T.CC[:, o:o + 28], T.R16[:, o:o + 28], T.SL[:, n + 28:n + 56], A.add, ["R16%d" % h, sk], ["CC%d" % h])
        cp(T.OP[:, p:p + 56], T.CC[:, o:o + 56], ["CC%d" % h], ["OP%d" % h])
        idk = ["ID2a", "ID2b", "OP%d" % h]
        act(T.G2[:, 448 * h:448 * h + 448], T.ID2[:].indirect(T.OP[:, p + 28:p + 56]), AF.Copy, idk, ["G%d" % h])
        cp(T.CL[:, 448 * h:448 * h + 448], T.ID2[:].indirect(T.OP[:, p:p + 28]), idk, ["Hh%d" % h, "CL0s", "CL0v"])
        bank = "B%d" % (2 * h)
        for s in range(7):
            mm(T[bank][:, 0:64], T.ID[:], T.CL[:, 448 * h + 64 * s:448 * h + 64 * s + 64], s == 0, False, ["ID", "Hh%d" % h], [bank])
        for s in range(7):
            mm(T[bank][:, 0:64], T.ID[:], T.G2[:, 448 * h + 64 * s:448 * h + 64 * s + 64], False, s == 6, ["ID", "G%d" % h], [bank])

    weave(chain(columns, 0, 0), chain(lists), per=1)
    for t in range(TS):
        weave(chain(gathers, t, 0), chain(columns, t, 1), lead=1, per=5)
        gb = chain(gathers, t, 1)
        weave(gb[:2], [])
        weave(chain(escape, t, 0), [])
        weave(chain(choose, t, 0), [])
        weave(gb[2:3], chain(newz, t, 0))
        weave(gb[3:], [])
        weave(chain(spare, t), [])
        weave(chain(escape, t, 1), [])
        weave(chain(choose, t, 1), [])
        nxt = chain(columns, t + 1, 0) if t < TS - 1 else chain(partners, 0)
        weave(nxt[:2], chain(newz, t, 1), lead=1)
        weave(chain(write, t), nxt[2:])

    partners(1)
    act(T.YZ[:], T.ZF[:], AF.Identity, ["za0_%d" % TS, "za1_%d" % TS], ["YZ"], bias=-129.0)
    dma("S", T.yz[:], T.YZ[:], ["YZ"], ["o2"], "out2")
    act(T.YF[:], T.ID2[:].indirect(T.OP[:, 128:136]), AF.Copy, ["ID2a", "ID2b", "OPf0", "OPf1"], ["YF"])
    dma("S", T.yf[:], T.YF[0:128:16, :], ["YF"], ["o2"], "out2")
    for h in range(2):
        ts(T.YP[:, 64 * h:64 * h + 64], T["B%d" % (2 * h)][:, 0:64], col(0), None, A.add, None, ["B%d" % (2 * h), "c0"], ["YP"])
    dma("Y", T.yp[:], T.YP[:], ["YP"], ["o1"], "out")

    dsem, dcount = {}, {}
    lastw, readers = {}, {}
    for n, o in enumerate(ops):
        deps, after = set(), set()
        for k in o["r"]:
            for m in lastw.get(k, []):
                deps.add(m)
            if k[0] == "B" and len(k) == 2 and k[1].isdigit():
                deps.update(m for m in readers.get(k, []) if ops[m]["q"] != o["q"])
        for k in o["w"]:
            for m in readers.get(k, []) + lastw.get(k, []):
                same = ops[m]["q"] == o["q"] and ops[m]["dma"] is None and o["dma"] is None
                twin = o["dma"] is not None and ops[m]["dma"] == o["dma"]
                if not same and not twin and ops[m]["dma"] != "remote":
                    deps.add(m)
                elif same:
                    after.add(m)
        o["deps"] = deps if o["kind"] == "op" else set()
        o["after"] = after - deps - {n}
        for k in o["r"]:
            readers.setdefault(k, []).append(n)
        for k in o["w"]:
            if readers.get(k) or k not in lastw:
                lastw[k] = [n]
                readers[k] = []
            else:
                lastw[k] = lastw[k] + [n]
        if o["dma"] not in (None, "remote"):
            dsem.setdefault(o["dma"], "d%d" % len(dsem))
            dcount[o["dma"]] = dcount.get(o["dma"], 0) + 16
    def length(o):
        k = (o["w"] or [""])[0]
        if o["kind"] == "ext":
            return 0.0, 0.0
        if o["dma"] == "remote":
            return 0.3, FAR
        if o["dma"] is not None:
            return 0.1, 3.0
        if "cols" in o:
            c = o["cols"] * {"d": 0.0013, "a": 0.00104, "B": 0.0006}[k[0]] + (0.06 if k[0] == "d" else 0.0)
        elif o["q"] == "P":
            c = 0.1 if k == "B7" else 0.045
        elif o["q"] == "G":
            c = 1.8 if k[:2] == "W2" else 0.35
        else:
            c = 0.07
            r0 = (o["r"] or [""])[0]
            for pre, v in LENGTHS:
                if k.startswith(pre):
                    c = v
                    break
            if k[:2] == "ay":
                c = {"0": 0.47, "448": 0.34, "768": 0.14}[r0[4:]]
        return c, c

    sent = {o["sem"]: n for n, o in enumerate(ops) if o["dma"] == "remote"}
    succ = [[] for _ in ops]
    need = [0] * len(ops)
    lens = [length(o) for o in ops]
    for n, o in enumerate(ops):
        edges = [(m, lens[m][1] + WAKE) for m in o["deps"]] + [(m, lens[m][0]) for m in o["after"]]
        if o["kind"] == "ext":
            edges = [(sent[o["sem"]], FAR)]
        for m, lat in edges:
            succ[m].append((n, lat))
            need[n] += 1
    order, cnt0 = [n for n in range(len(ops)) if need[n] == 0], list(need)
    for n in order:
        for m, _ in succ[n]:
            cnt0[m] -= 1
            if cnt0[m] == 0:
                order.append(m)
    way = [0.0] * len(ops)
    for n in reversed(order):
        way[n] = max([lens[n][1]] + [lat + way[m] for m, lat in succ[n]])
        if ops[n]["dma"] == "remote" and (ops[n]["sem"][1:3] == "c0" or ops[n]["sem"] == "as0"):
            way[n] += LEAD
    ready, at, free, order = [n for n in range(len(ops)) if need[n] == 0], [0.0] * len(ops), {}, []
    while ready:
        start = {n: max(at[n], free.get(ops[n]["q"], 0.0)) for n in ready}
        first = min(ready, key=lambda n: (start[n], -way[n], n))
        q = ops[first]["q"]
        pick = max((n for n in ready if ops[n]["q"] == q and start[n] <= start[first] + SLACK), key=lambda n: (way[n], -n))
        ready.remove(pick)
        order.append(pick)
        if q is not None:
            free[q] = start[pick] + lens[pick][0]
        for m, lat in succ[pick]:
            at[m] = max(at[m], start[pick] + lat)
            need[m] -= 1
            if need[m] == 0:
                ready.append(m)
    place = {m: n for n, m in enumerate(order)}
    ops = [ops[m] for m in order]
    for o in ops:
        o["deps"] = {place[m] for m in o["deps"]}
    known = {q: {} for q in Q}
    for n, o in enumerate(ops):
        if o["kind"] != "op":
            o["clock"] = {}
            continue
        kn = known[o["q"]]
        best = {}
        for m in o["deps"]:
            d = ops[m]
            key = d["q"] if d["kind"] == "op" and d["dma"] is None else (d["dma"] if d["kind"] == "op" else d["sem"])
            best[key] = max(best.get(key, -1), m)
        o["waits"] = []
        for key, m in sorted(best.items(), key=lambda e: -e[1]):
            if kn.get(key, -1) >= m:
                continue
            o["waits"].append(m)
            ops[m]["inc"] = True
            d = ops[m]
            if d["kind"] == "op" and d["dma"] is not None:
                m = max(i for i, e in enumerate(ops) if e["dma"] == d["dma"])
            kn[key] = m
            for k2, v in d["clock"].items():
                kn[k2] = max(kn.get(k2, -1), v)
        o["clock"] = dict(kn)
    cnt = {q: 0 for q in Q}
    for o in ops:
        if o["kind"] == "op" and o["dma"] is None and o.get("inc"):
            cnt[o["q"]] += 1
            o["val"] = cnt[o["q"]]
    for o in ops:
        if o["kind"] != "op":
            continue
        q = Q[o["q"]]
        for m in o["waits"]:
            d = ops[m]
            if d["kind"] == "ext":
                q.wait_ge(T.sem[d["sem"]], d["n"])
            elif d["dma"] is None:
                q.wait_ge(T.sem["c" + d["q"]], d["val"])
            else:
                q.wait_ge(T.sem[dsem[d["dma"]]], dcount[d["dma"]])
        ins = o["fn"]()
        if o["dma"] is None:
            if o.get("inc"):
                ins.then_inc(T.sem["c" + o["q"]], 1)
        elif o["dma"] != "remote":
            ins.then_inc(T.sem[dsem[o["dma"]]], 16)
    g.wait_ge(T.sem.left, left[0])
    g.sync.wait_ge(T.sem[dsem["out"]], dcount["out"])
    g.scalar.wait_ge(T.sem[dsem["out2"]], dcount["out2"])
